import numpy as np
import ml_dtypes


def mxq(x, axis, fmt="e4m3"):
    dtype, down = {"e4m3": (ml_dtypes.float8_e4m3fn, 7), "e5m2": (ml_dtypes.float8_e5m2, 14)}[fmt]
    v = np.moveaxis(np.asarray(x, np.float32).astype(ml_dtypes.bfloat16).astype(np.float64), axis, -1)
    blocks = v.reshape(v.shape[:-1] + (-1, 32))
    amax = np.abs(blocks).max(-1, keepdims=True)
    byte = np.maximum(np.where(amax > 0, np.frexp(amax)[1] - 1 + 127, 0) - down, 1)
    scale = np.exp2(byte - 127.0)
    codes = (blocks / scale).astype(np.float32).astype(dtype).astype(np.float64)
    return np.moveaxis((codes * scale).reshape(v.shape), -1, axis)


WIDE = False


def mx_kscale(k):
    if not WIDE:
        return np.ones(k)
    levels = np.array([10, -10, 5, -5, 0])
    if k % 512:
        return np.exp2(np.random.permutation(np.resize(levels, k // 32))).repeat(32)
    a = np.empty((k // 512, 16))
    for p in range(k // 512):
        a[p, :8] = np.random.permutation(np.resize(levels, 8))
        for g in range(8):
            far = levels[np.abs(levels - a[p, g]) >= 10]
            a[p, g + 8] = far[np.random.randint(len(far))]
    return np.exp2(a.ravel()).repeat(32)


def f64(x):
    return np.asarray(x).astype(np.float64)


def striped(idx):
    return np.tile(idx.reshape(-1, 16).T, (8, 1)).astype(np.uint16)


def unstriped(offs):
    return offs[:16].T.reshape(-1).astype(np.int64)


E2M1 = np.array([0.0, 0.5, 1.0, 1.5, 2.0, 3.0, 4.0, 6.0, -0.0, -0.5, -1.0, -1.5, -2.0, -3.0, -4.0, -6.0])


def pack_weight(w, fmt):
    k, n = w.shape
    w = f64(np.asarray(w, np.float32).astype(ml_dtypes.bfloat16)).reshape(k // 32, 32, n)
    amax = np.abs(w).max(1)
    if fmt == "e4m3":
        byte = np.frexp(amax)[1] - 1 + 127 - 7
    else:
        mant, ex = np.frexp(amax / 6.0)
        byte = np.where(mant > 0.5, ex, ex - 1) + 127
    byte = np.clip(np.where(amax > 0, byte, 1), 1, 254)
    scaled = (w * np.exp2(127.0 - byte)[:, None, :]).reshape(k, n).astype(np.float32)
    by_word = np.ascontiguousarray(scaled.reshape(k // 512, 128, 4, n).transpose(0, 1, 3, 2))
    if fmt == "e4m3":
        words = by_word.astype(ml_dtypes.float8_e4m3fn).view(np.uint8)
    else:
        c = by_word.astype(ml_dtypes.float4_e2m1fn).view(np.uint8) & 0xF
        words = (c[..., 0::2] | (c[..., 1::2] << 4)).reshape(k // 512, 128, 2 * n)
    return np.ascontiguousarray(words), np.ascontiguousarray(byte.astype(np.uint8).reshape(k // 512, 16, n))


def unpack_weight(words, scales, fmt):
    g, _, n = scales.shape
    words = np.ascontiguousarray(words).reshape(g, 128, n, -1)
    if fmt == "e4m3":
        vals = words.view(ml_dtypes.float8_e4m3fn).astype(np.float64)
    else:
        nib = np.empty((g, 128, n, 4), np.uint8)
        nib[..., 0::2] = words & 0xF
        nib[..., 1::2] = words >> 4
        vals = E2M1[nib]
    vals = vals * np.repeat(np.exp2(scales.astype(np.float64) - 127.0), 8, axis=1)[..., None]
    return vals.transpose(0, 1, 3, 2).reshape(g * 512, n)


def relu(v):
    return np.maximum(v, 0.0)


K, T, E, C, H, N = 2048, 768, 2, 256, 512, 128
R = 2


def by_expert(wq, xq):
    return np.concatenate([wq[e].T @ xq[:, e * C:(e + 1) * C] for e in range(E)], axis=1)


def setup_inputs():
    n = np.random.standard_normal
    s = mx_kscale(K)[:, None]
    u = mx_kscale(H)
    slot_token = np.concatenate([r * (T // R) + np.random.permutation(T // R)[:C // R] for e in range(E) for r in range(R)])
    w1 = [pack_weight(m, "e2m1") for m in n((E, K, H)) / np.sqrt(K) / s[None]]
    w3 = [pack_weight(m, "e2m1") for m in n((E, K, H)) / np.sqrt(K) / s[None] * u[None, None, :]]
    w2 = [pack_weight(m, "e2m1") for m in n((E, H, N)) / np.sqrt(H) / u[None, :, None]]
    x = pack_weight(n((K, T)) * s, "e4m3")
    return {
        "x_words": x[0],
        "x_scales": x[1],
        "w1_words": np.stack([m[0] for m in w1]),
        "w1_scales": np.stack([m[1] for m in w1]),
        "w3_words": np.stack([m[0] for m in w3]),
        "w3_scales": np.stack([m[1] for m in w3]),
        "w2_words": np.stack([m[0] for m in w2]),
        "w2_scales": np.stack([m[1] for m in w2]),
        "offs": striped(slot_token),
    }


def reference(x_words, x_scales, w1_words, w1_scales, w3_words, w3_scales, w2_words, w2_scales, offs):
    idx = unstriped(offs)
    w1 = np.stack([unpack_weight(w1_words[e], w1_scales[e], "e2m1") for e in range(E)])
    w3 = np.stack([unpack_weight(w3_words[e], w3_scales[e], "e2m1") for e in range(E)])
    w2 = np.stack([unpack_weight(w2_words[e], w2_scales[e], "e2m1") for e in range(E)])
    xq = unpack_weight(x_words, x_scales, "e4m3")[:, idx]
    h = relu(by_expert(w1, xq))
    h = h * by_expert(w3, xq)
    y = by_expert(w2, mxq(h, 0, "e4m3"))
    return y.reshape(N, E, R, C // R).transpose(0, 2, 1, 3).reshape(N, E * C)

@@ -1,0 +1,195 @@
+from contextlib import ExitStack
+
+import concourse.mybir as mybir
+from concourse.masks import make_identity
+
+K, T, E, C, H, N = 2048, 768, 2, 256, 512, 128
+FLOPS = 2 * E * C * (2 * K * H + H * N)
+
+F32 = mybir.dt.float32
+BF16 = mybir.dt.bfloat16
+I32 = mybir.dt.int32
+U32 = mybir.dt.uint32
+U16 = mybir.dt.uint16
+U8 = mybir.dt.uint8
+FP8X4 = mybir.dt.float8_e4m3fn_x4
+FP4X4 = mybir.dt.float4_e2m1fn_x4
+RELU = mybir.ActivationFunctionType.Relu
+MULT = mybir.AluOpType.mult
+
+P = 128
+PASSES = 4
+SLOTS = E * C
+TILES = SLOTS // P
+
+
+def tile_moe_pke_glu_relu_kernel(
+    tc, x_words, x_scales, w1_words, w1_scales, w3_words, w3_scales, w2_words, w2_scales, offs, out
+):
+    nc = tc.nc
+    with ExitStack() as ctx:
+        keep = ctx.enter_context(tc.tile_pool(name="keep", bufs=1))
+        psum = ctx.enter_context(tc.psum_pool(name="psum", bufs=1))
+
+        offsets = keep.tile([P, SLOTS // 16], U16, name="offsets")
+        xw = [keep.tile([P, T], I32, name="xw%d" % s, align_bytes=64) for s in range(PASSES)]
+        xs = [keep.tile([P, 2 * T], U8, name="xs%d" % i, align_bytes=64) for i in range(2)]
+        s1 = keep.tile([P, E * PASSES * H], U8, name="s1", align_bytes=64)
+        s3 = keep.tile([P, E * PASSES * H], U8, name="s3", align_bytes=64)
+        s2 = keep.tile([P, E * N], U8, name="s2", align_bytes=64)
+        w1 = keep.tile([P, E * PASSES, 2 * H], U8, name="w1", align_bytes=64)
+        w3 = keep.tile([P, E * PASSES, 2 * H], U8, name="w3", align_bytes=64)
+        w2 = keep.tile([P, E, 2 * N], U8, name="w2", align_bytes=64)
+        gw = keep.tile([P, PASSES * SLOTS], U32, name="gw", align_bytes=64)
+        gs = keep.tile([P, PASSES * SLOTS], U8, name="gs", align_bytes=64)
+        ident = keep.tile([P, P], F32, name="ident", align_bytes=64)
+        a_ps = [psum.tile([P, H], F32, name="a%d" % t) for t in range(TILES)]
+        b_ps = [psum.tile([P, H], F32, name="b%d" % t) for t in range(TILES)]
+
+        def load_scales(queue, plane, src, groups):
+            rows = src.bitcast(I32)
+            width = rows.shape[2]
+            for r in range(4):
+                queue.dma_start(
+                    out=plane[:].bitcast(I32)[r:P:32, :].rearrange("q (g c) -> q g c", c=width),
+                    in_=rows[:, r:16:4, :].rearrange("g q c -> q g c"),
+                )
+
+        def load_x(s):
+            nc.sync.dma_start(out=xw[s][:], in_=x_words[s].rearrange("p t r -> p (t r)").bitcast(I32))
+
+        def load_w(dst, src, planes):
+            nc.sync.dma_start(
+                out=dst[:].bitcast(I32)[:, planes, :],
+                in_=src.bitcast(I32).rearrange("e s p c -> p (e s) c")[:, planes, :],
+            )
+
+        nc.gpsimd.memset(xs[0][:].bitcast(I32), 0)
+        for plane in (s1, xs[1], s3, s2):
+            nc.vector.memset(plane[:].bitcast(I32), 0)
+        make_identity(nc, ident[:])
+
+        def both(s):
+            return slice(s, E * PASSES, PASSES)
+
+        nc.sync.dma_start(offsets[:], offs)
+        load_x(0)
+        load_w(w1, w1_words, both(0))
+        load_scales(nc.sync, xs[0], x_scales[0:2], 2)
+        load_x(1)
+        load_scales(nc.sync, s1, w1_scales.rearrange("e s q c -> (e s) q c"), 8)
+        load_w(w1, w1_words, both(1))
+        load_w(w3, w3_words, both(0))
+        load_scales(nc.sync, xs[1], x_scales[2:4], 2)
+        load_scales(nc.sync, s3, w3_scales.rearrange("e s q c -> (e s) q c"), 8)
+        load_w(w3, w3_words, both(1))
+        load_x(2)
+        load_w(w1, w1_words, both(2))
+        load_x(3)
+        load_w(w1, w1_words, both(3))
+        load_w(w3, w3_words, slice(2, 4))
+        load_w(w3, w3_words, slice(6, 8))
+        load_scales(nc.sync, s2, w2_scales.rearrange("e s q c -> (e s) q c"), 2)
+        nc.sync.dma_start(out=w2[:].bitcast(I32), in_=w2_words.bitcast(I32).rearrange("e s p c -> p (e s) c"))
+        warm = keep.tile([P, 1], F32, name="warm")
+        nc.scalar.activation(warm[:], ident[:, 0:1], RELU)
+
+        def gather(dst, window, s, lo, hi):
+            nc.vector.tensor_copy(dst[:, s * SLOTS + lo : s * SLOTS + hi], window.indirect(offsets[:, lo // 16 : hi // 16]))
+
+        def gather_scales(s, lo=0, hi=SLOTS):
+            gather(gs, xs[s // 2][:, (s % 2) * T : (s % 2 + 1) * T], s, lo, hi)
+
+        def gather_words(s, lo, hi):
+            gather(gw, xw[s][:].bitcast(U32), s, lo, hi)
+
+        def mm(acc, words, plane, t, s):
+            g = (t // 2) * PASSES + s
+            cols = slice(s * SLOTS + t * P, s * SLOTS + (t + 1) * P)
+            nc.tensor.matmul_mx(
+                out=acc[t][:],
+                lhsT=gw[:, cols].bitcast(FP8X4),
+                lhsT_scale=gs[:, cols],
+                rhs=words[:, g, :].bitcast(FP4X4),
+                rhs_scale=plane[:, g * H : (g + 1) * H],
+                start=(s == 0),
+                stop=(s == PASSES - 1),
+            )
+
+        def mm_a(s, ts=range(TILES)):
+            for t in ts:
+                mm(a_ps, w1, s1, t, s)
+
+        def mm_b(s, ts=range(TILES)):
+            for t in ts:
+                mm(b_ps, w3, s3, t, s)
+
+        ra = [keep.tile([P, H], F32, name="ra%d" % t) for t in range(TILES)]
+        h = [keep.tile([P, H], BF16, name="h%d" % t, align_bytes=64) for t in range(TILES)]
+        ht = [keep.tile([P, H], BF16, name="ht%d" % t, align_bytes=64) for t in range(TILES)]
+        hq = [keep.tile([P, P], U32, name="hq%d" % t, align_bytes=64) for t in range(TILES)]
+        hs = [keep.tile([P, P], U8, name="hs%d" % t, align_bytes=64) for t in range(TILES)]
+        ys = [keep.tile([P, P], F32, name="ys%d" % t, align_bytes=64) for t in range(TILES)]
+
+        def split(ap):
+            return ap.rearrange("p (u m e) -> p u m e", u=2, e=2)
+
+        def perm(ap):
+            return ap.rearrange("p (m u e) -> p u m e", u=2, e=2)
+
+        def relu(t):
+            nc.scalar.activation(split(ra[t][:]), perm(a_ps[t][:]), RELU)
+
+        def mul(t):
+            nc.vector.tensor_tensor(split(h[t][:]), perm(b_ps[t][:]), split(ra[t][:]), MULT)
+
+        def turn(t):
+            words = h[t][:].bitcast(F32)
+            for u in range(2):
+                nc.tensor.transpose(a_ps[t][:, u * P : (u + 1) * P], words[:, u * P : (u + 1) * P], ident[:])
+
+        def lace(t):
+            nc.scalar.copy(
+                ht[t][:].bitcast(F32).rearrange("p (j u) -> p j u", u=2),
+                a_ps[t][:, 0 : 2 * P].rearrange("p (u j) -> p j u", u=2),
+            )
+
+        def quant(t):
+            nc.vector.quantize_mx(out=hq[t][:].bitcast(FP8X4), scales=hs[t][:], in_=ht[t][:])
+
+        def second(t):
+            e = t // 2
+            nc.tensor.matmul_mx(
+                out=b_ps[t][:, 0:P],
+                lhsT=w2[:, e, :].bitcast(FP4X4),
+                lhsT_scale=s2[:, e * N : (e + 1) * N],
+                rhs=hq[t][:].bitcast(FP8X4),
+                rhs_scale=hs[t][:],
+                start=True,
+                stop=True,
+            )
+
+        def store(t):
+            nc.scalar.copy(ys[t][:], b_ps[t][:, 0:P])
+            col = C * (t % 2) + P * (t // 2)
+            nc.sync.dma_start(out=out[:, col : col + P], in_=ys[t][:])
+
+        for s in range(PASSES):
+            gather_scales(s)
+            gather_words(s, 0, C)
+            gather_words(s, C, SLOTS)
+            mm_a(s)
+            if 1 <= s <= 2:
+                mm_b(s - 1)
+        for t in range(TILES):
+            relu(t)
+        for t in range(TILES):
+            mm_b(2, [t])
+            mm_b(3, [t])
+            mul(t)
+        for t in range(TILES):
+            turn(t)
+            lace(t)
+            quant(t)
+            second(t)
+            store(t)

@@ -29,19 +29,20 @@ def tile_moe_pke_glu_relu_kernel(
     nc = tc.nc
     with ExitStack() as ctx:
         keep = ctx.enter_context(tc.tile_pool(name="keep", bufs=1))
+        ring = ctx.enter_context(tc.tile_pool(name="ring", bufs=3))
         psum = ctx.enter_context(tc.psum_pool(name="psum", bufs=1))
 
         offsets = keep.tile([P, SLOTS // 16], U16, name="offsets")
         xw = [keep.tile([P, T], I32, name="xw%d" % s, align_bytes=64) for s in range(PASSES)]
-        xs = [keep.tile([P, 2 * T], U8, name="xs%d" % i, align_bytes=64) for i in range(2)]
+        xs = keep.tile([P, PASSES * T], U8, name="xs", align_bytes=64)
         s1 = keep.tile([P, E * PASSES * H], U8, name="s1", align_bytes=64)
         s3 = keep.tile([P, E * PASSES * H], U8, name="s3", align_bytes=64)
         s2 = keep.tile([P, E * N], U8, name="s2", align_bytes=64)
-        w1 = keep.tile([P, E * PASSES, 2 * H], U8, name="w1", align_bytes=64)
-        w3 = keep.tile([P, E * PASSES, 2 * H], U8, name="w3", align_bytes=64)
+        w1 = [keep.tile([P, E, 2 * H], U8, name="w1_%d" % s, align_bytes=64) for s in range(PASSES)]
+        w3 = [keep.tile([P, E, 2 * H], U8, name="w3_%d" % s, align_bytes=64) for s in range(PASSES)]
         w2 = keep.tile([P, E, 2 * N], U8, name="w2", align_bytes=64)
-        gw = keep.tile([P, PASSES * SLOTS], U32, name="gw", align_bytes=64)
-        gs = keep.tile([P, PASSES * SLOTS], U8, name="gs", align_bytes=64)
+        gw = {}
+        gs = {}
         ident = keep.tile([P, P], F32, name="ident", align_bytes=64)
         a_ps = [psum.tile([P, H], F32, name="a%d" % t) for t in range(TILES)]
         b_ps = [psum.tile([P, H], F32, name="b%d" % t) for t in range(TILES)]
@@ -58,59 +59,69 @@ def tile_moe_pke_glu_relu_kernel(
         def load_x(s):
             nc.sync.dma_start(out=xw[s][:], in_=x_words[s].rearrange("p t r -> p (t r)").bitcast(I32))
 
-        def load_w(dst, src, planes):
-            nc.sync.dma_start(
-                out=dst[:].bitcast(I32)[:, planes, :],
-                in_=src.bitcast(I32).rearrange("e s p c -> p (e s) c")[:, planes, :],
-            )
+        def load_w(dst, src, s):
+            nc.sync.dma_start(out=dst[s][:].bitcast(I32), in_=src.bitcast(I32)[:, s].rearrange("e p c -> p e c"))
 
-        nc.gpsimd.memset(xs[0][:].bitcast(I32), 0)
-        for plane in (s1, xs[1], s3, s2):
-            nc.vector.memset(plane[:].bitcast(I32), 0)
-        make_identity(nc, ident[:])
-
-        def both(s):
-            return slice(s, E * PASSES, PASSES)
+        zeros = keep.tile([P, 4 * H], BF16, name="zeros", align_bytes=64)
+        zq = keep.tile([P, H], U32, name="zq", align_bytes=64)
+        zs = keep.tile([P, H], U8, name="zs", align_bytes=64)
+        nc.vector.memset(xs[:].bitcast(I32), 0)
+        nc.vector.memset(s1[:].bitcast(I32), 0)
+        nc.gpsimd.memset(s3[:].bitcast(I32), 0)
+        nc.gpsimd.memset(zeros[:].bitcast(I32), 0)
+        nc.vector.memset(s2[:].bitcast(I32), 0)
+        nc.vector.quantize_mx(out=zq[:].bitcast(FP8X4), scales=zs[:], in_=zeros[:])
 
         nc.sync.dma_start(offsets[:], offs)
         load_x(0)
-        load_w(w1, w1_words, both(0))
-        load_scales(nc.sync, xs[0], x_scales[0:2], 2)
+        load_w(w1, w1_words, 0)
+        load_scales(nc.sync, xs, x_scales, PASSES)
         load_x(1)
         load_scales(nc.sync, s1, w1_scales.rearrange("e s q c -> (e s) q c"), 8)
-        load_w(w1, w1_words, both(1))
-        load_w(w3, w3_words, both(0))
-        load_scales(nc.sync, xs[1], x_scales[2:4], 2)
+        load_w(w3, w3_words, 0)
         load_scales(nc.sync, s3, w3_scales.rearrange("e s q c -> (e s) q c"), 8)
-        load_w(w3, w3_words, both(1))
+        make_identity(nc, ident[:])
+        load_w(w1, w1_words, 1)
         load_x(2)
-        load_w(w1, w1_words, both(2))
+        load_w(w3, w3_words, 1)
+        load_w(w1, w1_words, 2)
         load_x(3)
-        load_w(w1, w1_words, both(3))
-        load_w(w3, w3_words, slice(2, 4))
-        load_w(w3, w3_words, slice(6, 8))
+        load_w(w3, w3_words, 2)
+        load_w(w1, w1_words, 3)
+        load_w(w3, w3_words, 3)
         load_scales(nc.sync, s2, w2_scales.rearrange("e s q c -> (e s) q c"), 2)
         nc.sync.dma_start(out=w2[:].bitcast(I32), in_=w2_words.bitcast(I32).rearrange("e s p c -> p (e s) c"))
-        warm = keep.tile([P, 1], F32, name="warm")
-        nc.scalar.activation(warm[:], ident[:, 0:1], RELU)
+        for i in range(4):
+            nc.tensor.matmul_mx(
+                out=b_ps[i % TILES][:],
+                lhsT=zq[:, 0:P].bitcast(FP8X4),
+                lhsT_scale=zs[:, 0:P],
+                rhs=w1[0][:, 0, :].bitcast(FP4X4),
+                rhs_scale=zs[:],
+                start=True,
+                stop=True,
+            )
 
         def gather(dst, window, s, lo, hi):
             nc.vector.tensor_copy(dst[:, s * SLOTS + lo : s * SLOTS + hi], window.indirect(offsets[:, lo // 16 : hi // 16]))
 
         def gather_scales(s, lo=0, hi=SLOTS):
-            gather(gs, xs[s // 2][:, (s % 2) * T : (s % 2 + 1) * T], s, lo, hi)
+            if s not in gs:
+                gs[s] = ring.tile([P, SLOTS], U8, name="gs", align_bytes=64)
+            gather(gs[s], xs[:, s * T : (s + 1) * T], 0, lo, hi)
 
         def gather_words(s, lo, hi):
-            gather(gw, xw[s][:].bitcast(U32), s, lo, hi)
+            if s not in gw:
+                gw[s] = ring.tile([P, SLOTS], U32, name="gw", align_bytes=64)
+            gather(gw[s], xw[s][:].bitcast(U32), 0, lo, hi)
 
         def mm(acc, words, plane, t, s):
             g = (t // 2) * PASSES + s
-            cols = slice(s * SLOTS + t * P, s * SLOTS + (t + 1) * P)
             nc.tensor.matmul_mx(
                 out=acc[t][:],
-                lhsT=gw[:, cols].bitcast(FP8X4),
-                lhsT_scale=gs[:, cols],
-                rhs=words[:, g, :].bitcast(FP4X4),
+                lhsT=gw[s][:, t * P : (t + 1) * P].bitcast(FP8X4),
+                lhsT_scale=gs[s][:, t * P : (t + 1) * P],
+                rhs=words[s][:, t // 2, :].bitcast(FP4X4),
                 rhs_scale=plane[:, g * H : (g + 1) * H],
                 start=(s == 0),
                 stop=(s == PASSES - 1),
@@ -175,17 +186,25 @@ def tile_moe_pke_glu_relu_kernel(
             nc.sync.dma_start(out=out[:, col : col + P], in_=ys[t][:])
 
         for s in range(PASSES):
-            gather_scales(s)
-            gather_words(s, 0, C)
-            gather_words(s, C, SLOTS)
-            mm_a(s)
-            if 1 <= s <= 2:
-                mm_b(s - 1)
+            if s == 0:
+                for lo in (0, C):
+                    gather_scales(s, lo, lo + C)
+                    gather_words(s, lo, lo + C)
+            else:
+                gather_scales(s)
+                gather_words(s, 0, C)
+                gather_words(s, C, SLOTS)
+            if s < PASSES - 1:
+                mm_a(s)
+                mm_b(s)
+        last = PASSES - 1
+        mm_a(last, [0])
+        relu(0)
         for t in range(TILES):
-            relu(t)
-        for t in range(TILES):
-            mm_b(2, [t])
-            mm_b(3, [t])
+            if t + 1 < TILES:
+                mm_a(last, [t + 1])
+                relu(t + 1)
+            mm_b(last, [t])
             mul(t)
         for t in range(TILES):
             turn(t)

@@ -62,14 +62,12 @@ def tile_moe_pke_glu_relu_kernel(
         def load_w(dst, src, s):
             nc.sync.dma_start(out=dst[s][:].bitcast(I32), in_=src.bitcast(I32)[:, s].rearrange("e p c -> p e c"))
 
-        zeros = keep.tile([P, 4 * H], BF16, name="zeros", align_bytes=64)
-        zq = keep.tile([P, H], U32, name="zq", align_bytes=64)
-        zs = keep.tile([P, H], U8, name="zs", align_bytes=64)
-        nc.vector.memset(xs[:].bitcast(I32), 0)
-        nc.vector.memset(s1[:].bitcast(I32), 0)
-        nc.gpsimd.memset(s3[:].bitcast(I32), 0)
-        nc.gpsimd.memset(zeros[:].bitcast(I32), 0)
-        nc.vector.memset(s2[:].bitcast(I32), 0)
+        zeros = keep.tile([P, 2 * H], BF16, name="zeros", align_bytes=64)
+        zq = keep.tile([P, 2 * P], U32, name="zq", align_bytes=64)
+        zs = keep.tile([P, 2 * P], U8, name="zs", align_bytes=64)
+        nc.gpsimd.memset(xs[:].bitcast(I32), 0)
+        for plane in (s1, s3, s2, zeros):
+            nc.vector.memset(plane[:].bitcast(I32), 0)
         nc.vector.quantize_mx(out=zq[:].bitcast(FP8X4), scales=zs[:], in_=zeros[:])
 
         nc.sync.dma_start(offsets[:], offs)
@@ -91,12 +89,12 @@ def tile_moe_pke_glu_relu_kernel(
         load_w(w3, w3_words, 3)
         load_scales(nc.sync, s2, w2_scales.rearrange("e s q c -> (e s) q c"), 2)
         nc.sync.dma_start(out=w2[:].bitcast(I32), in_=w2_words.bitcast(I32).rearrange("e s p c -> p (e s) c"))
-        for i in range(4):
+        for i in range(8):
             nc.tensor.matmul_mx(
-                out=b_ps[i % TILES][:],
+                out=b_ps[i % TILES][:, 0 : 2 * P],
                 lhsT=zq[:, 0:P].bitcast(FP8X4),
                 lhsT_scale=zs[:, 0:P],
-                rhs=w1[0][:, 0, :].bitcast(FP4X4),
+                rhs=w1[0][:, 0, 0:H].bitcast(FP4X4),
                 rhs_scale=zs[:],
                 start=True,
                 stop=True,
@@ -142,22 +140,16 @@ def tile_moe_pke_glu_relu_kernel(
         hs = [keep.tile([P, P], U8, name="hs%d" % t, align_bytes=64) for t in range(TILES)]
         ys = [keep.tile([P, P], F32, name="ys%d" % t, align_bytes=64) for t in range(TILES)]
 
-        def split(ap):
-            return ap.rearrange("p (u m e) -> p u m e", u=2, e=2)
-
-        def perm(ap):
-            return ap.rearrange("p (m u e) -> p u m e", u=2, e=2)
-
         def relu(t):
-            nc.scalar.activation(split(ra[t][:]), perm(a_ps[t][:]), RELU)
+            nc.scalar.activation(ra[t][:], a_ps[t][:], RELU)
 
         def mul(t):
-            nc.vector.tensor_tensor(split(h[t][:]), perm(b_ps[t][:]), split(ra[t][:]), MULT)
+            nc.vector.tensor_tensor(h[t][:], b_ps[t][:], ra[t][:], MULT)
 
         def turn(t):
             words = h[t][:].bitcast(F32)
             for u in range(2):
-                nc.tensor.transpose(a_ps[t][:, u * P : (u + 1) * P], words[:, u * P : (u + 1) * P], ident[:])
+                nc.tensor.transpose(a_ps[t][:, u * P : (u + 1) * P], words[:, u : 2 * P : 2], ident[:])
 
         def lace(t):
             nc.scalar.copy(
@@ -192,8 +184,9 @@ def tile_moe_pke_glu_relu_kernel(
                     gather_words(s, lo, lo + C)
             else:
                 gather_scales(s)
-                gather_words(s, 0, C)
-                gather_words(s, C, SLOTS)
+                step = P if s == PASSES - 1 else C
+                for lo in range(0, SLOTS, step):
+                    gather_words(s, lo, lo + step)
             if s < PASSES - 1:
                 mm_a(s)
                 mm_b(s)

@@ -18,9 +18,16 @@ RELU = mybir.ActivationFunctionType.Relu
 MULT = mybir.AluOpType.mult
 
 P = 128
-PASSES = 4
+PASSES = K // 512
+RANKS = 2
 SLOTS = E * C
 TILES = SLOTS // P
+LIST_ROWS = 16
+SCALE_ROWS = 16
+QUADRANT = 32
+FP4_BYTES = 2
+HALF = PASSES // 2
+ALIGN = 64
 
 
 def tile_moe_pke_glu_relu_kernel(
@@ -29,179 +36,141 @@ def tile_moe_pke_glu_relu_kernel(
     nc = tc.nc
     with ExitStack() as ctx:
         keep = ctx.enter_context(tc.tile_pool(name="keep", bufs=1))
-        ring = ctx.enter_context(tc.tile_pool(name="ring", bufs=3))
         psum = ctx.enter_context(tc.psum_pool(name="psum", bufs=1))
 
-        offsets = keep.tile([P, SLOTS // 16], U16, name="offsets")
-        xw = [keep.tile([P, T], I32, name="xw%d" % s, align_bytes=64) for s in range(PASSES)]
-        xs = keep.tile([P, PASSES * T], U8, name="xs", align_bytes=64)
-        s1 = keep.tile([P, E * PASSES * H], U8, name="s1", align_bytes=64)
-        s3 = keep.tile([P, E * PASSES * H], U8, name="s3", align_bytes=64)
-        s2 = keep.tile([P, E * N], U8, name="s2", align_bytes=64)
-        w1 = [keep.tile([P, E, 2 * H], U8, name="w1_%d" % s, align_bytes=64) for s in range(PASSES)]
-        w3 = [keep.tile([P, E, 2 * H], U8, name="w3_%d" % s, align_bytes=64) for s in range(PASSES)]
-        w2 = keep.tile([P, E, 2 * N], U8, name="w2", align_bytes=64)
-        gw = {}
-        gs = {}
-        ident = keep.tile([P, P], F32, name="ident", align_bytes=64)
-        a_ps = [psum.tile([P, H], F32, name="a%d" % t) for t in range(TILES)]
-        b_ps = [psum.tile([P, H], F32, name="b%d" % t) for t in range(TILES)]
+        def sbuf(shape, dtype, name):
+            return keep.tile(shape, dtype, name=name, align_bytes=ALIGN)
 
-        def load_scales(queue, plane, src, groups):
-            rows = src.bitcast(I32)
-            width = rows.shape[2]
-            for r in range(4):
-                queue.dma_start(
-                    out=plane[:].bitcast(I32)[r:P:32, :].rearrange("q (g c) -> q g c", c=width),
-                    in_=rows[:, r:16:4, :].rearrange("g q c -> q g c"),
+        offsets = keep.tile([P, SLOTS // LIST_ROWS], U16, name="offsets")
+        x_w = [sbuf([P, T], I32, "x_w%d" % s) for s in range(PASSES)]
+        x_s = [sbuf([P, HALF * T], U8, "x_s%d" % half) for half in range(2)]
+        w1_s = sbuf([P, E * PASSES * H], U8, "w1_s")
+        w3_s = sbuf([P, E * PASSES * H], U8, "w3_s")
+        w2_s = sbuf([P, E * N], U8, "w2_s")
+        w1_w = [sbuf([P, E, FP4_BYTES * H], U8, "w1_w%d" % s) for s in range(PASSES)]
+        w3_early = [sbuf([P, E, FP4_BYTES * H], U8, "w3_early%d" % s) for s in range(HALF)]
+        w3_late = [sbuf([P, HALF, FP4_BYTES * H], U8, "w3_late%d" % e) for e in range(E)]
+        w2_w = sbuf([P, E, FP4_BYTES * N], U8, "w2_w")
+        slot_w = sbuf([P, PASSES * SLOTS], U32, "slot_w")
+        slot_s = sbuf([P, PASSES * SLOTS], U8, "slot_s")
+        ident = sbuf([P, P], F32, "ident")
+        a_bank = [psum.tile([P, H], F32, name="a_bank%d" % t) for t in range(TILES)]
+        b_bank = [psum.tile([P, H], F32, name="b_bank%d" % t) for t in range(TILES)]
+
+        nc.gpsimd.memset(x_s[0][:].bitcast(I32), 0)
+        for plane in (w1_s, x_s[1], w3_s, w2_s):
+            nc.vector.memset(plane[:].bitcast(I32), 0)
+        make_identity(nc, ident[:])
+
+        def load_scales(plane, rows):
+            words = rows.bitcast(I32)
+            for r in range(SCALE_ROWS // 4):
+                nc.sync.dma_start(
+                    out=plane[:].bitcast(I32)[r:P:QUADRANT, :].rearrange("q (g c) -> q g c", c=words.shape[2]),
+                    in_=words[:, r:SCALE_ROWS:4, :].rearrange("g q c -> q g c"),
                 )
 
-        def load_x(s):
-            nc.sync.dma_start(out=xw[s][:], in_=x_words[s].rearrange("p t r -> p (t r)").bitcast(I32))
+        def load_weight_scales(plane, scales):
+            load_scales(plane, scales.rearrange("e s q c -> (e s) q c"))
 
-        def load_w(dst, src, s):
-            nc.sync.dma_start(out=dst[s][:].bitcast(I32), in_=src.bitcast(I32)[:, s].rearrange("e p c -> p e c"))
+        def load_tokens(s):
+            nc.sync.dma_start(out=x_w[s][:], in_=x_words[s].rearrange("p t r -> p (t r)").bitcast(I32))
 
-        zeros = keep.tile([P, 2 * H], BF16, name="zeros", align_bytes=64)
-        zq = keep.tile([P, 2 * P], U32, name="zq", align_bytes=64)
-        zs = keep.tile([P, 2 * P], U8, name="zs", align_bytes=64)
-        nc.gpsimd.memset(xs[:].bitcast(I32), 0)
-        for plane in (s1, s3, s2, zeros):
-            nc.vector.memset(plane[:].bitcast(I32), 0)
-        nc.vector.quantize_mx(out=zq[:].bitcast(FP8X4), scales=zs[:], in_=zeros[:])
+        def load_words(tile, rows):
+            nc.sync.dma_start(out=tile[:].bitcast(I32), in_=rows.bitcast(I32).rearrange("g p c -> p g c"))
 
         nc.sync.dma_start(offsets[:], offs)
-        load_x(0)
-        load_w(w1, w1_words, 0)
-        load_scales(nc.sync, xs, x_scales, PASSES)
-        load_x(1)
-        load_scales(nc.sync, s1, w1_scales.rearrange("e s q c -> (e s) q c"), 8)
-        load_w(w3, w3_words, 0)
-        load_scales(nc.sync, s3, w3_scales.rearrange("e s q c -> (e s) q c"), 8)
-        make_identity(nc, ident[:])
-        load_w(w1, w1_words, 1)
-        load_x(2)
-        load_w(w3, w3_words, 1)
-        load_w(w1, w1_words, 2)
-        load_x(3)
-        load_w(w3, w3_words, 2)
-        load_w(w1, w1_words, 3)
-        load_w(w3, w3_words, 3)
-        load_scales(nc.sync, s2, w2_scales.rearrange("e s q c -> (e s) q c"), 2)
-        nc.sync.dma_start(out=w2[:].bitcast(I32), in_=w2_words.bitcast(I32).rearrange("e s p c -> p (e s) c"))
-        for i in range(8):
+        load_tokens(0)
+        load_words(w1_w[0], w1_words[:, 0])
+        load_scales(x_s[0], x_scales[0:HALF])
+        load_tokens(1)
+        load_weight_scales(w1_s, w1_scales)
+        load_words(w1_w[1], w1_words[:, 1])
+        load_words(w3_early[0], w3_words[:, 0])
+        load_scales(x_s[1], x_scales[HALF:PASSES])
+        load_weight_scales(w3_s, w3_scales)
+        load_words(w3_early[1], w3_words[:, 1])
+        for s in range(HALF, PASSES):
+            load_tokens(s)
+            load_words(w1_w[s], w1_words[:, s])
+        for e in range(E):
+            load_words(w3_late[e], w3_words[e, HALF:PASSES])
+        load_weight_scales(w2_s, w2_scales)
+        load_words(w2_w, w2_words[:, 0])
+
+        def gather(dst, window, s, first, last):
+            entries = offsets[:, first // LIST_ROWS : last // LIST_ROWS]
+            nc.vector.tensor_copy(dst[:, s * SLOTS + first : s * SLOTS + last], window.indirect(entries))
+
+        def first_product(bank, words, plane, t, s):
+            group = (t // RANKS) * PASSES + s
+            slots = slice(s * SLOTS + t * P, s * SLOTS + (t + 1) * P)
             nc.tensor.matmul_mx(
-                out=b_ps[i % TILES][:, 0 : 2 * P],
-                lhsT=zq[:, 0:P].bitcast(FP8X4),
-                lhsT_scale=zs[:, 0:P],
-                rhs=w1[0][:, 0, 0:H].bitcast(FP4X4),
-                rhs_scale=zs[:],
-                start=True,
-                stop=True,
-            )
-
-        def gather(dst, window, s, lo, hi):
-            nc.vector.tensor_copy(dst[:, s * SLOTS + lo : s * SLOTS + hi], window.indirect(offsets[:, lo // 16 : hi // 16]))
-
-        def gather_scales(s, lo=0, hi=SLOTS):
-            if s not in gs:
-                gs[s] = ring.tile([P, SLOTS], U8, name="gs", align_bytes=64)
-            gather(gs[s], xs[:, s * T : (s + 1) * T], 0, lo, hi)
-
-        def gather_words(s, lo, hi):
-            if s not in gw:
-                gw[s] = ring.tile([P, SLOTS], U32, name="gw", align_bytes=64)
-            gather(gw[s], xw[s][:].bitcast(U32), 0, lo, hi)
-
-        def mm(acc, words, plane, t, s):
-            g = (t // 2) * PASSES + s
-            nc.tensor.matmul_mx(
-                out=acc[t][:],
-                lhsT=gw[s][:, t * P : (t + 1) * P].bitcast(FP8X4),
-                lhsT_scale=gs[s][:, t * P : (t + 1) * P],
-                rhs=words[s][:, t // 2, :].bitcast(FP4X4),
-                rhs_scale=plane[:, g * H : (g + 1) * H],
+                out=bank[:],
+                lhsT=slot_w[:, slots].bitcast(FP8X4),
+                lhsT_scale=slot_s[:, slots],
+                rhs=words.bitcast(FP4X4),
+                rhs_scale=plane[:, group * H : (group + 1) * H],
                 start=(s == 0),
                 stop=(s == PASSES - 1),
             )
 
-        def mm_a(s, ts=range(TILES)):
-            for t in ts:
-                mm(a_ps, w1, s1, t, s)
+        def pass_a(t, s):
+            first_product(a_bank[t], w1_w[s][:, t // RANKS, :], w1_s, t, s)
 
-        def mm_b(s, ts=range(TILES)):
-            for t in ts:
-                mm(b_ps, w3, s3, t, s)
+        def pass_b(t, s):
+            e = t // RANKS
+            words = w3_early[s][:, e, :] if s < HALF else w3_late[e][:, s - HALF, :]
+            first_product(b_bank[t], words, w3_s, t, s)
 
-        ra = [keep.tile([P, H], F32, name="ra%d" % t) for t in range(TILES)]
-        h = [keep.tile([P, H], BF16, name="h%d" % t, align_bytes=64) for t in range(TILES)]
-        ht = [keep.tile([P, H], BF16, name="ht%d" % t, align_bytes=64) for t in range(TILES)]
-        hq = [keep.tile([P, P], U32, name="hq%d" % t, align_bytes=64) for t in range(TILES)]
-        hs = [keep.tile([P, P], U8, name="hs%d" % t, align_bytes=64) for t in range(TILES)]
-        ys = [keep.tile([P, P], F32, name="ys%d" % t, align_bytes=64) for t in range(TILES)]
+        def by_pairs(ap):
+            return ap.rearrange("p (u m v) -> p u m v", u=2, v=2)
 
-        def relu(t):
-            nc.scalar.activation(ra[t][:], a_ps[t][:], RELU)
+        def from_i_order(ap):
+            return ap.rearrange("p (m u v) -> p u m v", u=2, v=2)
 
-        def mul(t):
-            nc.vector.tensor_tensor(h[t][:], b_ps[t][:], ra[t][:], MULT)
+        relu_a = [keep.tile([P, H], F32, name="relu_a%d" % t) for t in range(TILES)]
+        h = [sbuf([P, H], BF16, "h%d" % t) for t in range(TILES)]
+        h_turned = [sbuf([P, H], BF16, "h_turned%d" % t) for t in range(TILES)]
+        h_w = [sbuf([P, P], U32, "h_w%d" % t) for t in range(TILES)]
+        h_s = [sbuf([P, P], U8, "h_s%d" % t) for t in range(TILES)]
+        y = [sbuf([P, P], F32, "y%d" % t) for t in range(TILES)]
 
-        def turn(t):
-            words = h[t][:].bitcast(F32)
+        for s in range(PASSES):
+            gather(slot_s, x_s[s // HALF][:, (s % HALF) * T : (s % HALF + 1) * T], s, 0, SLOTS)
+            for e in range(E):
+                gather(slot_w, x_w[s][:].bitcast(U32), s, e * C, (e + 1) * C)
+            for t in range(TILES):
+                pass_a(t, s)
+            if 1 <= s <= HALF:
+                for t in range(TILES):
+                    pass_b(t, s - 1)
+        for t in range(TILES):
+            nc.scalar.activation(by_pairs(relu_a[t][:]), from_i_order(a_bank[t][:]), RELU)
+        for t in range(TILES):
+            for s in range(HALF, PASSES):
+                pass_b(t, s)
+            nc.vector.tensor_tensor(by_pairs(h[t][:]), from_i_order(b_bank[t][:]), by_pairs(relu_a[t][:]), MULT)
+
+        for t in range(TILES):
+            e, rank = divmod(t, RANKS)
+            pairs = h[t][:].bitcast(F32)
             for u in range(2):
-                nc.tensor.transpose(a_ps[t][:, u * P : (u + 1) * P], words[:, u : 2 * P : 2], ident[:])
-
-        def lace(t):
+                nc.tensor.transpose(a_bank[t][:, u * P : (u + 1) * P], pairs[:, u * P : (u + 1) * P], ident[:])
             nc.scalar.copy(
-                ht[t][:].bitcast(F32).rearrange("p (j u) -> p j u", u=2),
-                a_ps[t][:, 0 : 2 * P].rearrange("p (u j) -> p j u", u=2),
+                h_turned[t][:].bitcast(F32).rearrange("p (j u) -> p j u", u=2),
+                a_bank[t][:, 0 : 2 * P].rearrange("p (u j) -> p j u", u=2),
             )
-
-        def quant(t):
-            nc.vector.quantize_mx(out=hq[t][:].bitcast(FP8X4), scales=hs[t][:], in_=ht[t][:])
-
-        def second(t):
-            e = t // 2
+            nc.vector.quantize_mx(out=h_w[t][:].bitcast(FP8X4), scales=h_s[t][:], in_=h_turned[t][:])
             nc.tensor.matmul_mx(
-                out=b_ps[t][:, 0:P],
-                lhsT=w2[:, e, :].bitcast(FP4X4),
-                lhsT_scale=s2[:, e * N : (e + 1) * N],
-                rhs=hq[t][:].bitcast(FP8X4),
-                rhs_scale=hs[t][:],
+                out=b_bank[t][:, 0:P],
+                lhsT=w2_w[:, e, :].bitcast(FP4X4),
+                lhsT_scale=w2_s[:, e * N : (e + 1) * N],
+                rhs=h_w[t][:].bitcast(FP8X4),
+                rhs_scale=h_s[t][:],
                 start=True,
                 stop=True,
             )
-
-        def store(t):
-            nc.scalar.copy(ys[t][:], b_ps[t][:, 0:P])
-            col = C * (t % 2) + P * (t // 2)
-            nc.sync.dma_start(out=out[:, col : col + P], in_=ys[t][:])
-
-        for s in range(PASSES):
-            if s == 0:
-                for lo in (0, C):
-                    gather_scales(s, lo, lo + C)
-                    gather_words(s, lo, lo + C)
-            else:
-                gather_scales(s)
-                step = P if s == PASSES - 1 else C
-                for lo in range(0, SLOTS, step):
-                    gather_words(s, lo, lo + step)
-            if s < PASSES - 1:
-                mm_a(s)
-                mm_b(s)
-        last = PASSES - 1
-        mm_a(last, [0])
-        relu(0)
-        for t in range(TILES):
-            if t + 1 < TILES:
-                mm_a(last, [t + 1])
-                relu(t + 1)
-            mm_b(last, [t])
-            mul(t)
-        for t in range(TILES):
-            turn(t)
-            lace(t)
-            quant(t)
-            second(t)
-            store(t)
+            nc.scalar.copy(y[t][:], b_bank[t][:, 0:P])
+            column = (rank * E + e) * P
+            nc.sync.dma_start(out=out[:, column : column + P], in_=y[t][:])

@@ -27,6 +27,8 @@ SCALE_ROWS = 16
 QUADRANT = 32
 FP4_BYTES = 2
 HALF = PASSES // 2
+LIVE_SPAN = 3 * QUADRANT + 4
+BELOW = 16
 ALIGN = 64
 
 
@@ -43,85 +45,72 @@ def tile_moe_pke_glu_relu_kernel(
 
         offsets = keep.tile([P, SLOTS // LIST_ROWS], U16, name="offsets")
         x_w = [sbuf([P, T], I32, "x_w%d" % s) for s in range(PASSES)]
-        x_s = [sbuf([P, HALF * T], U8, "x_s%d" % half) for half in range(2)]
-        w1_s = sbuf([P, E * PASSES * H], U8, "w1_s")
-        w3_s = sbuf([P, E * PASSES * H], U8, "w3_s")
-        w2_s = sbuf([P, E * N], U8, "w2_s")
-        w1_w = [sbuf([P, E, FP4_BYTES * H], U8, "w1_w%d" % s) for s in range(PASSES)]
-        w3_early = [sbuf([P, E, FP4_BYTES * H], U8, "w3_early%d" % s) for s in range(HALF)]
-        w3_late = [sbuf([P, HALF, FP4_BYTES * H], U8, "w3_late%d" % e) for e in range(E)]
-        w2_w = sbuf([P, E, FP4_BYTES * N], U8, "w2_w")
+        x_s = [sbuf([P, T], U8, "x_s%d" % j) for j in range(HALF)]
         slot_w = sbuf([P, PASSES * SLOTS], U32, "slot_w")
-        slot_s = sbuf([P, PASSES * SLOTS], U8, "slot_s")
+        slot_s = [sbuf([P, HALF * SLOTS], U8, "slot_s%d" % odd) for odd in range(2)]
+        w2_s = sbuf([P, E * N], U8, "w2_s")
+        w2_w = sbuf([P, E, FP4_BYTES * N], U8, "w2_w")
         ident = sbuf([P, P], F32, "ident")
         a_bank = [psum.tile([P, H], F32, name="a_bank%d" % t) for t in range(TILES)]
         b_bank = [psum.tile([P, H], F32, name="b_bank%d" % t) for t in range(TILES)]
+        words_of = {}
+        scales_of = {}
 
-        nc.gpsimd.memset(x_s[0][:].bitcast(I32), 0)
-        for plane in (w1_s, x_s[1], w3_s, w2_s):
-            nc.vector.memset(plane[:].bitcast(I32), 0)
-        make_identity(nc, ident[:])
+        def zero(engine, plane):
+            engine.memset(plane[:].bitcast(I32), 0)
 
-        def load_scales(plane, rows):
-            words = rows.bitcast(I32)
+        def weight_plane(name, experts, passes):
+            plane = sbuf([P, len(experts), len(passes) * H], U8, "%s_s%d%d" % (name, experts[0], passes[0]))
+            for i, e in enumerate(experts):
+                for j, s in enumerate(passes):
+                    scales_of[name, e, s] = plane[:, i, j * H : (j + 1) * H]
+            return plane
+
+        def load_scale_rows(queue, plane, rows):
             for r in range(SCALE_ROWS // 4):
-                nc.sync.dma_start(
-                    out=plane[:].bitcast(I32)[r:P:QUADRANT, :].rearrange("q (g c) -> q g c", c=words.shape[2]),
-                    in_=words[:, r:SCALE_ROWS:4, :].rearrange("g q c -> q g c"),
+                queue.dma_start(
+                    out=plane.bitcast(I32)[r:P:QUADRANT],
+                    in_=rows.bitcast(I32)[:, r:SCALE_ROWS:4, :].rearrange("g q c -> q g c"),
                 )
-
-        def load_weight_scales(plane, scales):
-            load_scales(plane, scales.rearrange("e s q c -> (e s) q c"))
 
         def load_tokens(s):
             nc.sync.dma_start(out=x_w[s][:], in_=x_words[s].rearrange("p t r -> p (t r)").bitcast(I32))
 
-        def load_words(tile, rows):
+        def load_words(name, source, groups):
+            tile = sbuf([P, len(groups), FP4_BYTES * H], U8, "%s_w%d%d" % (name, groups[0][0], groups[0][1]))
+            if len(groups) == 1:
+                rows = source[groups[0][0], groups[0][1] : groups[0][1] + 1]
+            elif groups[0][0] == groups[1][0]:
+                rows = source[groups[0][0], groups[0][1] : groups[-1][1] + 1 : groups[1][1] - groups[0][1]]
+            else:
+                rows = source[:, groups[0][1]]
             nc.sync.dma_start(out=tile[:].bitcast(I32), in_=rows.bitcast(I32).rearrange("g p c -> p g c"))
+            for i, (e, s) in enumerate(groups):
+                words_of[name, e, s] = tile[:, i, :]
 
-        nc.sync.dma_start(offsets[:], offs)
-        load_tokens(0)
-        load_words(w1_w[0], w1_words[:, 0])
-        load_scales(x_s[0], x_scales[0:HALF])
-        load_tokens(1)
-        load_weight_scales(w1_s, w1_scales)
-        load_words(w1_w[1], w1_words[:, 1])
-        load_words(w3_early[0], w3_words[:, 0])
-        load_scales(x_s[1], x_scales[HALF:PASSES])
-        load_weight_scales(w3_s, w3_scales)
-        load_words(w3_early[1], w3_words[:, 1])
-        for s in range(HALF, PASSES):
-            load_tokens(s)
-            load_words(w1_w[s], w1_words[:, s])
-        for e in range(E):
-            load_words(w3_late[e], w3_words[e, HALF:PASSES])
-        load_weight_scales(w2_s, w2_scales)
-        load_words(w2_w, w2_words[:, 0])
-
-        def gather(dst, window, s, first, last):
+        def gather(dst, window, first, last):
             entries = offsets[:, first // LIST_ROWS : last // LIST_ROWS]
-            nc.vector.tensor_copy(dst[:, s * SLOTS + first : s * SLOTS + last], window.indirect(entries))
+            nc.vector.tensor_copy(dst, window.indirect(entries))
 
-        def first_product(bank, words, plane, t, s):
-            group = (t // RANKS) * PASSES + s
-            slots = slice(s * SLOTS + t * P, s * SLOTS + (t + 1) * P)
+        def gather_words(s, first, last):
+            gather(slot_w[:, s * SLOTS + first : s * SLOTS + last], x_w[s][:].bitcast(U32), first, last)
+
+        def first_product(bank, name, t, s):
             nc.tensor.matmul_mx(
-                out=bank[:],
-                lhsT=slot_w[:, slots].bitcast(FP8X4),
-                lhsT_scale=slot_s[:, slots],
-                rhs=words.bitcast(FP4X4),
-                rhs_scale=plane[:, group * H : (group + 1) * H],
+                out=bank[t][:],
+                lhsT=slot_w[:, s * SLOTS + t * P : s * SLOTS + (t + 1) * P].bitcast(FP8X4),
+                lhsT_scale=slot_s[s % 2][:, (s // 2) * SLOTS + t * P : (s // 2) * SLOTS + (t + 1) * P],
+                rhs=words_of[name, t // RANKS, s].bitcast(FP4X4),
+                rhs_scale=scales_of[name, t // RANKS, s],
                 start=(s == 0),
                 stop=(s == PASSES - 1),
             )
 
         def pass_a(t, s):
-            first_product(a_bank[t], w1_w[s][:, t // RANKS, :], w1_s, t, s)
+            first_product(a_bank, "w1", t, s)
 
         def pass_b(t, s):
-            e = t // RANKS
-            words = w3_early[s][:, e, :] if s < HALF else w3_late[e][:, s - HALF, :]
-            first_product(b_bank[t], words, w3_s, t, s)
+            first_product(b_bank, "w3", t, s)
 
         def by_pairs(ap):
             return ap.rearrange("p (u m v) -> p u m v", u=2, v=2)
@@ -131,46 +120,135 @@ def tile_moe_pke_glu_relu_kernel(
 
         relu_a = [keep.tile([P, H], F32, name="relu_a%d" % t) for t in range(TILES)]
         h = [sbuf([P, H], BF16, "h%d" % t) for t in range(TILES)]
-        h_turned = [sbuf([P, H], BF16, "h_turned%d" % t) for t in range(TILES)]
-        h_w = [sbuf([P, P], U32, "h_w%d" % t) for t in range(TILES)]
-        h_s = [sbuf([P, P], U8, "h_s%d" % t) for t in range(TILES)]
-        y = [sbuf([P, P], F32, "y%d" % t) for t in range(TILES)]
 
-        for s in range(PASSES):
-            gather(slot_s, x_s[s // HALF][:, (s % HALF) * T : (s % HALF + 1) * T], s, 0, SLOTS)
-            for e in range(E):
-                gather(slot_w, x_w[s][:].bitcast(U32), s, e * C, (e + 1) * C)
-            for t in range(TILES):
-                pass_a(t, s)
-            if 1 <= s <= HALF:
-                for t in range(TILES):
-                    pass_b(t, s - 1)
-        for t in range(TILES):
+        def relu(t):
             nc.scalar.activation(by_pairs(relu_a[t][:]), from_i_order(a_bank[t][:]), RELU)
-        for t in range(TILES):
-            for s in range(HALF, PASSES):
-                pass_b(t, s)
+
+        def product(t):
             nc.vector.tensor_tensor(by_pairs(h[t][:]), from_i_order(b_bank[t][:]), by_pairs(relu_a[t][:]), MULT)
 
-        for t in range(TILES):
-            e, rank = divmod(t, RANKS)
-            pairs = h[t][:].bitcast(F32)
-            for u in range(2):
-                nc.tensor.transpose(a_bank[t][:, u * P : (u + 1) * P], pairs[:, u * P : (u + 1) * P], ident[:])
-            nc.scalar.copy(
-                h_turned[t][:].bitcast(F32).rearrange("p (j u) -> p j u", u=2),
-                a_bank[t][:, 0 : 2 * P].rearrange("p (u j) -> p j u", u=2),
+        quantised = {}
+
+        def turn(tiles, copier):
+            first, count = tiles[0], len(tiles)
+            for i, t in enumerate(tiles):
+                pairs = h[t][:].bitcast(F32)
+                for u in range(2):
+                    column = (2 * i + u) * P
+                    nc.tensor.transpose(a_bank[first][:, column : column + P], pairs[:, u * P : (u + 1) * P], ident[:])
+            turned = sbuf([P, count * H], BF16, "h_turned%d" % first)
+            copier(
+                turned[:].bitcast(F32).rearrange("p (i j u) -> p i j u", i=count, u=2),
+                a_bank[first][:, 0 : count * 2 * P].rearrange("p (i u j) -> p i j u", i=count, u=2),
             )
-            nc.vector.quantize_mx(out=h_w[t][:].bitcast(FP8X4), scales=h_s[t][:], in_=h_turned[t][:])
+            h_w = sbuf([P, count * P], U32, "h_w%d" % first)
+            h_s = sbuf([P, count * P], U8, "h_s%d" % first)
+            nc.vector.quantize_mx(out=h_w[:].bitcast(FP8X4), scales=h_s[:], in_=turned[:])
+            quantised[first] = (h_w, h_s)
+
+        def second_product(tiles, copier, queue):
+            first, count = tiles[0], len(tiles)
+            e, rank = divmod(first, RANKS)
+            h_w, h_s = quantised[first]
             nc.tensor.matmul_mx(
-                out=b_bank[t][:, 0:P],
+                out=b_bank[first][:, 0 : count * P],
                 lhsT=w2_w[:, e, :].bitcast(FP4X4),
                 lhsT_scale=w2_s[:, e * N : (e + 1) * N],
-                rhs=h_w[t][:].bitcast(FP8X4),
-                rhs_scale=h_s[t][:],
+                rhs=h_w[:].bitcast(FP8X4),
+                rhs_scale=h_s[:],
                 start=True,
                 stop=True,
             )
-            nc.scalar.copy(y[t][:], b_bank[t][:, 0:P])
-            column = (rank * E + e) * P
-            nc.sync.dma_start(out=out[:, column : column + P], in_=y[t][:])
+            y = sbuf([P, count, P], F32, "y%d" % first)
+            copier(y[:], b_bank[first][:, 0 : count * P].rearrange("p (i j) -> p i j", i=count))
+            by_rank = out.rearrange("n (r e u) -> n r e u", r=RANKS, e=E)
+            queue.dma_start(out=by_rank[:, rank : rank + count, e, :], in_=y[:])
+
+        def load_token_scales(j):
+            for r in range(SCALE_ROWS // 4):
+                nc.sync.dma_start(
+                    out=x_s[j][:].bitcast(I32)[r:P:BELOW, :],
+                    in_=x_scales.bitcast(I32)[2 * j : 2 * j + 2, r:SCALE_ROWS:4, :].rearrange("s q c -> q s c"),
+                )
+
+        def gather_scales(j):
+            gather(slot_s[0][:, j * SLOTS : (j + 1) * SLOTS], x_s[j][:], 0, SLOTS)
+
+        def load_weight_scales(queue, plane, source, experts, passes):
+            step = passes[1] - passes[0]
+            groups = source.rearrange("e s q c -> (e s) q c")
+            rows = groups[experts[0] * PASSES + passes[0] : (experts[-1] + 1) * PASSES : step]
+            load_scale_rows(queue, plane[:].rearrange("p e (s c) -> p (e s) c", c=H), rows)
+
+        def move_scales_up(queue):
+            queue.dma_start(
+                out=slot_s[1][:].bitcast(I32)[0:LIVE_SPAN, :],
+                in_=slot_s[0][:].bitcast(I32)[BELOW : BELOW + LIVE_SPAN, :],
+            )
+
+        def load_w2(queue, scale_queue):
+            load_scale_rows(
+                scale_queue, w2_s[:].rearrange("p (e c) -> p e c", e=E), w2_scales.rearrange("e s q c -> (e s) q c")
+            )
+            queue.dma_start(out=w2_w[:].bitcast(I32), in_=w2_words[:, 0].bitcast(I32).rearrange("g p c -> p g c"))
+
+        both, early, late, every = [0, 1], [0, 2], [1, 3], [0, 1, 2, 3]
+        w1_plane = weight_plane("w1", both, every)
+        w3_plane = weight_plane("w3", both, every)
+        for plane in x_s:
+            zero(nc.gpsimd, plane)
+        for plane in (w1_plane, w3_plane, slot_s[1], w2_s):
+            zero(nc.vector, plane)
+        make_identity(nc, ident[:])
+
+        def by_pass(s):
+            return [(e, s) for e in both]
+
+        def by_expert(e, passes):
+            return [(e, s) for s in passes]
+
+        nc.sync.dma_start(offsets[:], offs)
+        load_token_scales(0)
+        load_tokens(0)
+        load_words("w1", w1_words, by_pass(0))
+        load_weight_scales(nc.sync, w1_plane, w1_scales, both, every)
+        load_weight_scales(nc.gpsimd, w3_plane, w3_scales, both, every)
+        load_tokens(2)
+        load_token_scales(1)
+        load_words("w1", w1_words, by_pass(2))
+        load_words("w3", w3_words, by_pass(0))
+        load_words("w3", w3_words, by_pass(2))
+        load_tokens(1)
+        load_words("w1", w1_words, by_pass(1))
+        load_tokens(3)
+        load_words("w1", w1_words, by_pass(3))
+        for e in both:
+            load_words("w3", w3_words, by_expert(e, late))
+        load_w2(nc.sync, nc.sync)
+
+        def gather_and_pass_a(s):
+            for e in both:
+                gather_words(s, e * C, (e + 1) * C)
+            for t in range(TILES):
+                pass_a(t, s)
+
+        for s in early:
+            gather_scales(s // 2)
+            gather_and_pass_a(s)
+        move_scales_up(nc.scalar)
+        for s in early:
+            for t in range(TILES):
+                pass_b(t, s)
+        for s in late:
+            gather_and_pass_a(s)
+        for t in range(TILES):
+            relu(t)
+        for t in range(TILES):
+            for s in late:
+                pass_b(t, s)
+            product(t)
+        groups = [[0, 1], [2], [3]]
+        for tiles in groups:
+            turn(tiles, nc.scalar.copy)
+        for tiles in groups:
+            second_product(tiles, nc.scalar.copy, nc.sync)

@@ -40,14 +40,14 @@ def tile_moe_pke_glu_relu_kernel(
         keep = ctx.enter_context(tc.tile_pool(name="keep", bufs=1))
         psum = ctx.enter_context(tc.psum_pool(name="psum", bufs=1))
 
-        def sbuf(shape, dtype, name):
-            return keep.tile(shape, dtype, name=name, align_bytes=ALIGN)
+        def sbuf(shape, dtype, name, tag=None):
+            return keep.tile(shape, dtype, name=name, tag=tag or name, align_bytes=ALIGN)
 
         offsets = keep.tile([P, SLOTS // LIST_ROWS], U16, name="offsets")
         x_w = [sbuf([P, T], I32, "x_w%d" % s) for s in range(PASSES)]
-        x_s = [sbuf([P, T], U8, "x_s%d" % j) for j in range(HALF)]
+        x_s = sbuf([P, HALF * T], U8, "x_s")
         slot_w = sbuf([P, PASSES * SLOTS], U32, "slot_w")
-        slot_s = [sbuf([P, HALF * SLOTS], U8, "slot_s%d" % odd) for odd in range(2)]
+        slot_s = {s: sbuf([P, SLOTS], U8, "slot_s%d" % s) for s in (0, 2, 3)}
         w2_s = sbuf([P, E * N], U8, "w2_s")
         w2_w = sbuf([P, E, FP4_BYTES * N], U8, "w2_w")
         ident = sbuf([P, P], F32, "ident")
@@ -66,8 +66,8 @@ def tile_moe_pke_glu_relu_kernel(
                     scales_of[name, e, s] = plane[:, i, j * H : (j + 1) * H]
             return plane
 
-        def load_scale_rows(queue, plane, rows):
-            for r in range(SCALE_ROWS // 4):
+        def load_scale_rows(queue, plane, rows, which=range(SCALE_ROWS // 4)):
+            for r in which:
                 queue.dma_start(
                     out=plane.bitcast(I32)[r:P:QUADRANT],
                     in_=rows.bitcast(I32)[:, r:SCALE_ROWS:4, :].rearrange("g q c -> q g c"),
@@ -76,8 +76,9 @@ def tile_moe_pke_glu_relu_kernel(
         def load_tokens(s):
             nc.sync.dma_start(out=x_w[s][:], in_=x_words[s].rearrange("p t r -> p (t r)").bitcast(I32))
 
-        def load_words(name, source, groups):
-            tile = sbuf([P, len(groups), FP4_BYTES * H], U8, "%s_w%d%d" % (name, groups[0][0], groups[0][1]))
+        def load_words(name, source, groups, tile=None):
+            if tile is None:
+                tile = sbuf([P, len(groups), FP4_BYTES * H], U8, "%s_w%d%d" % (name, groups[0][0], groups[0][1]))
             if len(groups) == 1:
                 rows = source[groups[0][0], groups[0][1] : groups[0][1] + 1]
             elif groups[0][0] == groups[1][0]:
@@ -99,7 +100,7 @@ def tile_moe_pke_glu_relu_kernel(
             nc.tensor.matmul_mx(
                 out=bank[t][:],
                 lhsT=slot_w[:, s * SLOTS + t * P : s * SLOTS + (t + 1) * P].bitcast(FP8X4),
-                lhsT_scale=slot_s[s % 2][:, (s // 2) * SLOTS + t * P : (s // 2) * SLOTS + (t + 1) * P],
+                lhsT_scale=slot_s[s][:, t * P : (t + 1) * P],
                 rhs=words_of[name, t // RANKS, s].bitcast(FP4X4),
                 rhs_scale=scales_of[name, t // RANKS, s],
                 start=(s == 0),
@@ -164,15 +165,15 @@ def tile_moe_pke_glu_relu_kernel(
             by_rank = out.rearrange("n (r e u) -> n r e u", r=RANKS, e=E)
             queue.dma_start(out=by_rank[:, rank : rank + count, e, :], in_=y[:])
 
-        def load_token_scales(j):
-            for r in range(SCALE_ROWS // 4):
+        def load_token_scales(rows):
+            for r in rows:
                 nc.sync.dma_start(
-                    out=x_s[j][:].bitcast(I32)[r:P:BELOW, :],
-                    in_=x_scales.bitcast(I32)[2 * j : 2 * j + 2, r:SCALE_ROWS:4, :].rearrange("s q c -> q s c"),
+                    out=x_s[:].bitcast(I32)[r:P:BELOW, :].rearrange("p (j c) -> p j c", j=HALF),
+                    in_=x_scales.bitcast(I32)[:, r:SCALE_ROWS:4, :].rearrange("s q c -> q s c"),
                 )
 
-        def gather_scales(j):
-            gather(slot_s[0][:, j * SLOTS : (j + 1) * SLOTS], x_s[j][:], 0, SLOTS)
+        def gather_scales(j, first, last):
+            gather(slot_s[j][:, first:last], x_s[:, j * T : (j + 1) * T], first, last)
 
         def load_weight_scales(queue, plane, source, experts, passes):
             step = passes[1] - passes[0]
@@ -180,10 +181,10 @@ def tile_moe_pke_glu_relu_kernel(
             rows = groups[experts[0] * PASSES + passes[0] : (experts[-1] + 1) * PASSES : step]
             load_scale_rows(queue, plane[:].rearrange("p e (s c) -> p (e s) c", c=H), rows)
 
-        def move_scales_up(queue):
+        def move_scales_up(queue, s):
             queue.dma_start(
-                out=slot_s[1][:].bitcast(I32)[0:LIVE_SPAN, :],
-                in_=slot_s[0][:].bitcast(I32)[BELOW : BELOW + LIVE_SPAN, :],
+                out=slot_s[s][:].bitcast(I32)[0:LIVE_SPAN, :],
+                in_=slot_s[s - HALF][:].bitcast(I32)[BELOW : BELOW + LIVE_SPAN, :],
             )
 
         def load_w2(queue, scale_queue):
@@ -192,14 +193,28 @@ def tile_moe_pke_glu_relu_kernel(
             )
             queue.dma_start(out=w2_w[:].bitcast(I32), in_=w2_words[:, 0].bitcast(I32).rearrange("g p c -> p g c"))
 
-        both, early, late, every = [0, 1], [0, 2], [1, 3], [0, 1, 2, 3]
+        both, early, late, every = [0, 1], [0, 1], [2, 3], [0, 1, 2, 3]
         w1_plane = weight_plane("w1", both, every)
         w3_plane = weight_plane("w3", both, every)
-        for plane in x_s:
+        for plane in (x_s, w3_plane):
             zero(nc.gpsimd, plane)
-        for plane in (w1_plane, w3_plane, slot_s[1], w2_s):
+        for plane in (w1_plane, slot_s[2], slot_s[3], w2_s):
             zero(nc.vector, plane)
         make_identity(nc, ident[:])
+        w3_last = sbuf([P, HALF, FP4_BYTES * H], U8, "w3_last")
+        last_slots = slot_w[:, (PASSES - 1) * SLOTS : (PASSES - 1) * SLOTS + P]
+        nc.vector.memset(w3_last[:, 0, :].bitcast(I32), 0)
+        nc.vector.memset(last_slots.bitcast(I32), 0)
+        for warm_up in range(4):
+            nc.tensor.matmul_mx(
+                out=b_bank[TILES - 1][:],
+                lhsT=last_slots.bitcast(FP8X4),
+                lhsT_scale=slot_s[3][:, 0:P],
+                rhs=w3_last[:, 0, :].bitcast(FP4X4),
+                rhs_scale=slot_s[3][:],
+                start=True,
+                stop=True,
+            )
 
         def by_pass(s):
             return [(e, s) for e in both]
@@ -208,47 +223,63 @@ def tile_moe_pke_glu_relu_kernel(
             return [(e, s) for s in passes]
 
         nc.sync.dma_start(offsets[:], offs)
-        load_token_scales(0)
+        load_token_scales(range(4))
         load_tokens(0)
         load_words("w1", w1_words, by_pass(0))
         load_weight_scales(nc.sync, w1_plane, w1_scales, both, every)
-        load_weight_scales(nc.gpsimd, w3_plane, w3_scales, both, every)
-        load_tokens(2)
-        load_token_scales(1)
-        load_words("w1", w1_words, by_pass(2))
         load_words("w3", w3_words, by_pass(0))
-        load_words("w3", w3_words, by_pass(2))
         load_tokens(1)
+        load_weight_scales(nc.sync, w3_plane, w3_scales, both, every)
         load_words("w1", w1_words, by_pass(1))
-        load_tokens(3)
-        load_words("w1", w1_words, by_pass(3))
+        load_words("w3", w3_words, by_pass(1))
+        load_tokens(2)
         for e in both:
-            load_words("w3", w3_words, by_expert(e, late))
+            gather_scales(0, e * C, (e + 1) * C)
+        for t in range(TILES):
+            gather_words(0, t * P, (t + 1) * P)
+        slot_s[1] = sbuf([P, SLOTS], U8, "slot_s1", tag="x_w0")
+        for e in both:
+            gather_scales(1, e * C, (e + 1) * C)
+            gather_words(1, e * C, (e + 1) * C)
+        move_scales_up(nc.sync, 2)
+        load_words("w1", w1_words, by_expert(0, late))
+        load_tokens(3)
+        load_words("w3", w3_words, by_expert(0, late))
+        move_scales_up(nc.sync, 3)
+        load_words("w1", w1_words, by_expert(1, late))
+        load_words("w3", w3_words, by_expert(1, late), w3_last)
         load_w2(nc.sync, nc.sync)
 
-        def gather_and_pass_a(s):
+        for s in late:
             for e in both:
                 gather_words(s, e * C, (e + 1) * C)
+        for one_pass in (pass_a, pass_b):
             for t in range(TILES):
-                pass_a(t, s)
-
-        for s in early:
-            gather_scales(s // 2)
-            gather_and_pass_a(s)
-        move_scales_up(nc.scalar)
-        for s in early:
-            for t in range(TILES):
-                pass_b(t, s)
+                one_pass(t, 0)
+        for tiles in ((0, 1), (2, 3)):
+            for one_pass in (pass_a, pass_b):
+                for t in tiles:
+                    one_pass(t, 1)
         for s in late:
-            gather_and_pass_a(s)
-        for t in range(TILES):
+            for t in (0, 1):
+                pass_a(t, s)
+            for t in (0, 1):
+                pass_b(t, s)
+        for t in (0, 1):
             relu(t)
-        for t in range(TILES):
+            product(t)
+        for s in late:
+            for t in (2, 3):
+                pass_a(t, s)
+        for t in (2, 3):
+            relu(t)
+        turn([0, 1], nc.scalar.copy)
+        for t in (2, 3):
             for s in late:
                 pass_b(t, s)
             product(t)
-        groups = [[0, 1], [2], [3]]
-        for tiles in groups:
-            turn(tiles, nc.scalar.copy)
-        for tiles in groups:
-            second_product(tiles, nc.scalar.copy, nc.sync)
+        second_product([0, 1], nc.scalar.copy, nc.sync)
+        for t in (2, 3):
+            turn([t], nc.scalar.copy)
+        for t in (2, 3):
+            second_product([t], nc.scalar.copy, nc.sync)

@@ -40,14 +40,14 @@ def tile_moe_pke_glu_relu_kernel(
         keep = ctx.enter_context(tc.tile_pool(name="keep", bufs=1))
         psum = ctx.enter_context(tc.psum_pool(name="psum", bufs=1))
 
-        def sbuf(shape, dtype, name, tag=None):
-            return keep.tile(shape, dtype, name=name, tag=tag or name, align_bytes=ALIGN)
+        def sbuf(shape, dtype, name):
+            return keep.tile(shape, dtype, name=name, align_bytes=ALIGN)
 
         offsets = keep.tile([P, SLOTS // LIST_ROWS], U16, name="offsets")
         x_w = [sbuf([P, T], I32, "x_w%d" % s) for s in range(PASSES)]
         x_s = sbuf([P, HALF * T], U8, "x_s")
         slot_w = sbuf([P, PASSES * SLOTS], U32, "slot_w")
-        slot_s = {s: sbuf([P, SLOTS], U8, "slot_s%d" % s) for s in (0, 2, 3)}
+        slot_s = [sbuf([P, HALF * SLOTS], U8, "slot_s%d" % odd) for odd in range(2)]
         w2_s = sbuf([P, E * N], U8, "w2_s")
         w2_w = sbuf([P, E, FP4_BYTES * N], U8, "w2_w")
         ident = sbuf([P, P], F32, "ident")
@@ -66,8 +66,8 @@ def tile_moe_pke_glu_relu_kernel(
                     scales_of[name, e, s] = plane[:, i, j * H : (j + 1) * H]
             return plane
 
-        def load_scale_rows(queue, plane, rows, which=range(SCALE_ROWS // 4)):
-            for r in which:
+        def load_scale_rows(queue, plane, rows):
+            for r in range(SCALE_ROWS // 4):
                 queue.dma_start(
                     out=plane.bitcast(I32)[r:P:QUADRANT],
                     in_=rows.bitcast(I32)[:, r:SCALE_ROWS:4, :].rearrange("g q c -> q g c"),
@@ -76,9 +76,8 @@ def tile_moe_pke_glu_relu_kernel(
         def load_tokens(s):
             nc.sync.dma_start(out=x_w[s][:], in_=x_words[s].rearrange("p t r -> p (t r)").bitcast(I32))
 
-        def load_words(name, source, groups, tile=None):
-            if tile is None:
-                tile = sbuf([P, len(groups), FP4_BYTES * H], U8, "%s_w%d%d" % (name, groups[0][0], groups[0][1]))
+        def load_words(name, source, groups):
+            tile = sbuf([P, len(groups), FP4_BYTES * H], U8, "%s_w%d%d" % (name, groups[0][0], groups[0][1]))
             if len(groups) == 1:
                 rows = source[groups[0][0], groups[0][1] : groups[0][1] + 1]
             elif groups[0][0] == groups[1][0]:
@@ -100,7 +99,7 @@ def tile_moe_pke_glu_relu_kernel(
             nc.tensor.matmul_mx(
                 out=bank[t][:],
                 lhsT=slot_w[:, s * SLOTS + t * P : s * SLOTS + (t + 1) * P].bitcast(FP8X4),
-                lhsT_scale=slot_s[s][:, t * P : (t + 1) * P],
+                lhsT_scale=slot_s[s // HALF][:, (s % HALF) * SLOTS + t * P : (s % HALF) * SLOTS + (t + 1) * P],
                 rhs=words_of[name, t // RANKS, s].bitcast(FP4X4),
                 rhs_scale=scales_of[name, t // RANKS, s],
                 start=(s == 0),
@@ -173,7 +172,7 @@ def tile_moe_pke_glu_relu_kernel(
                 )
 
         def gather_scales(j, first, last):
-            gather(slot_s[j][:, first:last], x_s[:, j * T : (j + 1) * T], first, last)
+            gather(slot_s[0][:, j * SLOTS + first : j * SLOTS + last], x_s[:, j * T : (j + 1) * T], first, last)
 
         def load_weight_scales(queue, plane, source, experts, passes):
             step = passes[1] - passes[0]
@@ -181,40 +180,27 @@ def tile_moe_pke_glu_relu_kernel(
             rows = groups[experts[0] * PASSES + passes[0] : (experts[-1] + 1) * PASSES : step]
             load_scale_rows(queue, plane[:].rearrange("p e (s c) -> p (e s) c", c=H), rows)
 
-        def move_scales_up(queue, s):
+        def move_scales_up(queue):
             queue.dma_start(
-                out=slot_s[s][:].bitcast(I32)[0:LIVE_SPAN, :],
-                in_=slot_s[s - HALF][:].bitcast(I32)[BELOW : BELOW + LIVE_SPAN, :],
+                out=slot_s[1][:].bitcast(I32)[0:LIVE_SPAN, :],
+                in_=slot_s[0][:].bitcast(I32)[BELOW : BELOW + LIVE_SPAN, :],
             )
 
-        def load_w2(queue, scale_queue):
+        def load_w2_scales():
             load_scale_rows(
-                scale_queue, w2_s[:].rearrange("p (e c) -> p e c", e=E), w2_scales.rearrange("e s q c -> (e s) q c")
+                nc.sync, w2_s[:].rearrange("p (e c) -> p e c", e=E), w2_scales.rearrange("e s q c -> (e s) q c")
             )
-            queue.dma_start(out=w2_w[:].bitcast(I32), in_=w2_words[:, 0].bitcast(I32).rearrange("g p c -> p g c"))
+
+        def load_w2_words():
+            nc.sync.dma_start(out=w2_w[:].bitcast(I32), in_=w2_words[:, 0].bitcast(I32).rearrange("g p c -> p g c"))
 
         both, early, late, every = [0, 1], [0, 1], [2, 3], [0, 1, 2, 3]
         w1_plane = weight_plane("w1", both, every)
         w3_plane = weight_plane("w3", both, every)
-        for plane in (x_s, w3_plane):
-            zero(nc.gpsimd, plane)
-        for plane in (w1_plane, slot_s[2], slot_s[3], w2_s):
+        zero(nc.gpsimd, x_s)
+        for plane in (w1_plane, w3_plane, w2_s, slot_s[1]):
             zero(nc.vector, plane)
         make_identity(nc, ident[:])
-        w3_last = sbuf([P, HALF, FP4_BYTES * H], U8, "w3_last")
-        last_slots = slot_w[:, (PASSES - 1) * SLOTS : (PASSES - 1) * SLOTS + P]
-        nc.vector.memset(w3_last[:, 0, :].bitcast(I32), 0)
-        nc.vector.memset(last_slots.bitcast(I32), 0)
-        for warm_up in range(4):
-            nc.tensor.matmul_mx(
-                out=b_bank[TILES - 1][:],
-                lhsT=last_slots.bitcast(FP8X4),
-                lhsT_scale=slot_s[3][:, 0:P],
-                rhs=w3_last[:, 0, :].bitcast(FP4X4),
-                rhs_scale=slot_s[3][:],
-                start=True,
-                stop=True,
-            )
 
         def by_pass(s):
             return [(e, s) for e in both]
@@ -223,63 +209,42 @@ def tile_moe_pke_glu_relu_kernel(
             return [(e, s) for s in passes]
 
         nc.sync.dma_start(offsets[:], offs)
-        load_token_scales(range(4))
         load_tokens(0)
         load_words("w1", w1_words, by_pass(0))
-        load_weight_scales(nc.sync, w1_plane, w1_scales, both, every)
         load_words("w3", w3_words, by_pass(0))
-        load_tokens(1)
+        load_token_scales(range(4))
+        load_weight_scales(nc.sync, w1_plane, w1_scales, both, every)
         load_weight_scales(nc.sync, w3_plane, w3_scales, both, every)
+        load_w2_scales()
+        for j in range(HALF):
+            gather_scales(j, 0, SLOTS)
+        load_tokens(1)
         load_words("w1", w1_words, by_pass(1))
         load_words("w3", w3_words, by_pass(1))
-        load_tokens(2)
-        for e in both:
-            gather_scales(0, e * C, (e + 1) * C)
-        for t in range(TILES):
-            gather_words(0, t * P, (t + 1) * P)
-        slot_s[1] = sbuf([P, SLOTS], U8, "slot_s1", tag="x_w0")
-        for e in both:
-            gather_scales(1, e * C, (e + 1) * C)
-            gather_words(1, e * C, (e + 1) * C)
-        move_scales_up(nc.sync, 2)
-        load_words("w1", w1_words, by_expert(0, late))
-        load_tokens(3)
-        load_words("w3", w3_words, by_expert(0, late))
-        move_scales_up(nc.sync, 3)
-        load_words("w1", w1_words, by_expert(1, late))
-        load_words("w3", w3_words, by_expert(1, late), w3_last)
-        load_w2(nc.sync, nc.sync)
-
+        move_scales_up(nc.sync)
         for s in late:
+            load_tokens(s)
+            load_words("w1", w1_words, by_pass(s))
+        for e in both:
+            load_words("w3", w3_words, by_expert(e, late))
+        load_w2_words()
+
+        for s in every:
             for e in both:
                 gather_words(s, e * C, (e + 1) * C)
-        for one_pass in (pass_a, pass_b):
             for t in range(TILES):
-                one_pass(t, 0)
-        for tiles in ((0, 1), (2, 3)):
-            for one_pass in (pass_a, pass_b):
-                for t in tiles:
-                    one_pass(t, 1)
-        for s in late:
-            for t in (0, 1):
                 pass_a(t, s)
-            for t in (0, 1):
-                pass_b(t, s)
-        for t in (0, 1):
+            if s in early:
+                for t in range(TILES):
+                    pass_b(t, s)
+        for t in range(TILES):
             relu(t)
-            product(t)
-        for s in late:
-            for t in (2, 3):
-                pass_a(t, s)
-        for t in (2, 3):
-            relu(t)
-        turn([0, 1], nc.scalar.copy)
-        for t in (2, 3):
+        for t in range(TILES):
             for s in late:
                 pass_b(t, s)
             product(t)
-        second_product([0, 1], nc.scalar.copy, nc.sync)
-        for t in (2, 3):
-            turn([t], nc.scalar.copy)
-        for t in (2, 3):
-            second_product([t], nc.scalar.copy, nc.sync)
+        groups = [[0, 1], [2], [3]]
+        for tiles in groups:
+            turn(tiles, nc.scalar.copy)
+        for tiles in groups:
+            second_product(tiles, nc.scalar.copy, nc.sync)

@@ -129,17 +129,17 @@ def tile_moe_pke_glu_relu_kernel(
 
         quantised = {}
 
-        def turn(tiles, copier):
+        def turn(tiles, copier, bank):
             first, count = tiles[0], len(tiles)
             for i, t in enumerate(tiles):
                 pairs = h[t][:].bitcast(F32)
                 for u in range(2):
                     column = (2 * i + u) * P
-                    nc.tensor.transpose(a_bank[first][:, column : column + P], pairs[:, u * P : (u + 1) * P], ident[:])
+                    nc.tensor.transpose(bank[:, column : column + P], pairs[:, u * P : (u + 1) * P], ident[:])
             turned = sbuf([P, count * H], BF16, "h_turned%d" % first)
             copier(
                 turned[:].bitcast(F32).rearrange("p (i j u) -> p i j u", i=count, u=2),
-                a_bank[first][:, 0 : count * 2 * P].rearrange("p (i u j) -> p i j u", i=count, u=2),
+                bank[:, 0 : count * 2 * P].rearrange("p (i u j) -> p i j u", i=count, u=2),
             )
             h_w = sbuf([P, count * P], U32, "h_w%d" % first)
             h_s = sbuf([P, count * P], U8, "h_s%d" % first)
@@ -211,27 +211,34 @@ def tile_moe_pke_glu_relu_kernel(
         nc.sync.dma_start(offsets[:], offs)
         load_tokens(0)
         load_words("w1", w1_words, by_pass(0))
-        load_words("w3", w3_words, by_pass(0))
         load_token_scales(range(4))
         load_weight_scales(nc.sync, w1_plane, w1_scales, both, every)
+        load_words("w3", w3_words, by_pass(0))
         load_weight_scales(nc.sync, w3_plane, w3_scales, both, every)
-        load_w2_scales()
-        for j in range(HALF):
-            gather_scales(j, 0, SLOTS)
         load_tokens(1)
         load_words("w1", w1_words, by_pass(1))
         load_words("w3", w3_words, by_pass(1))
+        load_tokens(2)
+        for e in both:
+            gather_scales(0, e * C, (e + 1) * C)
+        gather_scales(1, 0, SLOTS)
         move_scales_up(nc.sync)
-        for s in late:
-            load_tokens(s)
-            load_words("w1", w1_words, by_pass(s))
+        last = PASSES - 1
+
+        def gather_pass(s, width):
+            for first in range(0, SLOTS, width):
+                gather_words(s, first, first + width)
+
+        load_words("w1", w1_words, by_pass(2))
+        load_tokens(last)
+        load_words("w1", w1_words, by_pass(last))
         for e in both:
             load_words("w3", w3_words, by_expert(e, late))
+        load_w2_scales()
         load_w2_words()
 
         for s in every:
-            for e in both:
-                gather_words(s, e * C, (e + 1) * C)
+            gather_pass(s, P if s == last else C)
             for t in range(TILES):
                 pass_a(t, s)
             if s in early:
@@ -245,6 +252,6 @@ def tile_moe_pke_glu_relu_kernel(
             product(t)
         groups = [[0, 1], [2], [3]]
         for tiles in groups:
-            turn(tiles, nc.scalar.copy)
+            turn(tiles, nc.scalar.copy, a_bank[tiles[0]])
         for tiles in groups:
             second_product(tiles, nc.scalar.copy, nc.sync)

@@ -230,28 +230,40 @@ def tile_moe_pke_glu_relu_kernel(
                 gather_words(s, first, first + width)
 
         load_words("w1", w1_words, by_pass(2))
+        load_words("w3", w3_words, [(0, 2)])
         load_tokens(last)
-        load_words("w1", w1_words, by_pass(last))
-        for e in both:
-            load_words("w3", w3_words, by_expert(e, late))
+        load_words("w1", w1_words, [(0, last)])
+        load_words("w3", w3_words, [(0, last)])
+        load_words("w1", w1_words, [(1, last)])
+        load_words("w3", w3_words, by_expert(1, late))
         load_w2_scales()
         load_w2_words()
 
         for s in every:
             gather_pass(s, P if s == last else C)
-            for t in range(TILES):
-                pass_a(t, s)
-            if s in early:
+        for s in early:
+            for one_pass in (pass_a, pass_b):
                 for t in range(TILES):
-                    pass_b(t, s)
+                    one_pass(t, s)
         for t in range(TILES):
+            pass_a(t, 2)
+        for t in (0, 1):
+            pass_b(t, 2)
+        for t in (0, 1):
+            pass_a(t, last)
             relu(t)
-        for t in range(TILES):
+        for t in (0, 1):
+            pass_b(t, last)
+            product(t)
+        for t in (2, 3):
+            pass_a(t, last)
+            relu(t)
+        for t in (2, 3):
             for s in late:
                 pass_b(t, s)
             product(t)
-        groups = [[0, 1], [2], [3]]
-        for tiles in groups:
-            turn(tiles, nc.scalar.copy, a_bank[tiles[0]])
-        for tiles in groups:
+        groups = [([0, 1], a_bank[2]), ([2], a_bank[0]), ([3], a_bank[1])]
+        for tiles, bank in groups:
+            turn(tiles, nc.scalar.copy, bank)
+        for tiles, bank in groups:
             second_product(tiles, nc.scalar.copy, nc.sync)

@@ -19,16 +19,18 @@ MULT = mybir.AluOpType.mult
 
 P = 128
 PASSES = K // 512
+LAST = PASSES - 1
+HALF = PASSES // 2
 RANKS = 2
 SLOTS = E * C
 TILES = SLOTS // P
 LIST_ROWS = 16
 SCALE_ROWS = 16
 QUADRANT = 32
-FP4_BYTES = 2
-HALF = PASSES // 2
-LIVE_SPAN = 3 * QUADRANT + 4
+GROUP_ROWS = 4
 BELOW = 16
+PLANE_SPAN = 3 * QUADRANT + GROUP_ROWS
+FP4_BYTES = 2
 ALIGN = 64
 
 
@@ -47,70 +49,115 @@ def tile_moe_pke_glu_relu_kernel(
         x_w = [sbuf([P, T], I32, "x_w%d" % s) for s in range(PASSES)]
         x_s = sbuf([P, HALF * T], U8, "x_s")
         slot_w = sbuf([P, PASSES * SLOTS], U32, "slot_w")
-        slot_s = [sbuf([P, HALF * SLOTS], U8, "slot_s%d" % odd) for odd in range(2)]
+        slot_s = [sbuf([P, HALF * SLOTS], U8, "slot_s%d" % pair) for pair in range(2)]
         w2_s = sbuf([P, E * N], U8, "w2_s")
         w2_w = sbuf([P, E, FP4_BYTES * N], U8, "w2_w")
         ident = sbuf([P, P], F32, "ident")
         a_bank = [psum.tile([P, H], F32, name="a_bank%d" % t) for t in range(TILES)]
         b_bank = [psum.tile([P, H], F32, name="b_bank%d" % t) for t in range(TILES)]
-        words_of = {}
-        scales_of = {}
+        relu_a = [keep.tile([P, H], F32, name="relu_a%d" % t) for t in range(TILES)]
+        h = [sbuf([P, H], BF16, "h%d" % t) for t in range(TILES)]
+        w1_s = sbuf([P, E * PASSES * H], U8, "w1_s")
+        w3_s = sbuf([P, E * PASSES * H], U8, "w3_s")
+        w1_w = {}
+        w3_w = {}
 
-        def zero(engine, plane):
-            engine.memset(plane[:].bitcast(I32), 0)
-
-        def weight_plane(name, experts, passes):
-            plane = sbuf([P, len(experts), len(passes) * H], U8, "%s_s%d%d" % (name, experts[0], passes[0]))
-            for i, e in enumerate(experts):
-                for j, s in enumerate(passes):
-                    scales_of[name, e, s] = plane[:, i, j * H : (j + 1) * H]
-            return plane
-
-        def load_scale_rows(queue, plane, rows):
-            for r in range(SCALE_ROWS // 4):
-                queue.dma_start(
-                    out=plane.bitcast(I32)[r:P:QUADRANT],
-                    in_=rows.bitcast(I32)[:, r:SCALE_ROWS:4, :].rearrange("g q c -> q g c"),
-                )
+        nc.gpsimd.memset(x_s[:].bitcast(I32), 0)
+        for plane in (w1_s, w3_s, w2_s, slot_s[1]):
+            nc.vector.memset(plane[:].bitcast(I32), 0)
+        make_identity(nc, ident[:])
 
         def load_tokens(s):
             nc.sync.dma_start(out=x_w[s][:], in_=x_words[s].rearrange("p t r -> p (t r)").bitcast(I32))
 
-        def load_words(name, source, groups):
+        def load_token_scales():
+            for r in range(GROUP_ROWS):
+                nc.sync.dma_start(
+                    out=x_s[:].bitcast(I32)[r:P:BELOW, :].rearrange("p (j c) -> p j c", j=HALF),
+                    in_=x_scales.bitcast(I32)[:, r:SCALE_ROWS:GROUP_ROWS, :].rearrange("s q c -> q s c"),
+                )
+
+        def load_weight_scales(plane, scales):
+            rows = scales.rearrange("e s q c -> (e s) q c").bitcast(I32)
+            for r in range(GROUP_ROWS):
+                nc.sync.dma_start(
+                    out=plane[:].bitcast(I32)[r:P:QUADRANT, :].rearrange("q (g c) -> q g c", c=rows.shape[2]),
+                    in_=rows[:, r:SCALE_ROWS:GROUP_ROWS, :].rearrange("g q c -> q g c"),
+                )
+
+        def load_words(name, loaded, rows, groups):
             tile = sbuf([P, len(groups), FP4_BYTES * H], U8, "%s_w%d%d" % (name, groups[0][0], groups[0][1]))
-            if len(groups) == 1:
-                rows = source[groups[0][0], groups[0][1] : groups[0][1] + 1]
-            elif groups[0][0] == groups[1][0]:
-                rows = source[groups[0][0], groups[0][1] : groups[-1][1] + 1 : groups[1][1] - groups[0][1]]
-            else:
-                rows = source[:, groups[0][1]]
             nc.sync.dma_start(out=tile[:].bitcast(I32), in_=rows.bitcast(I32).rearrange("g p c -> p g c"))
-            for i, (e, s) in enumerate(groups):
-                words_of[name, e, s] = tile[:, i, :]
+            for g, group in enumerate(groups):
+                loaded[group] = tile[:, g, :]
 
-        def gather(dst, window, first, last):
-            entries = offsets[:, first // LIST_ROWS : last // LIST_ROWS]
-            nc.vector.tensor_copy(dst, window.indirect(entries))
+        def load_pass(name, loaded, words, s):
+            load_words(name, loaded, words[:, s], [(e, s) for e in range(E)])
 
-        def gather_words(s, first, last):
-            gather(slot_w[:, s * SLOTS + first : s * SLOTS + last], x_w[s][:].bitcast(U32), first, last)
+        def load_expert(name, loaded, words, e, first, last):
+            load_words(name, loaded, words[e, first : last + 1], [(e, s) for s in range(first, last + 1)])
 
-        def first_product(bank, name, t, s):
+        def gather(dst, window, first, width):
+            entries = offsets[:, first // LIST_ROWS : (first + width) // LIST_ROWS]
+            nc.vector.tensor_copy(dst[:, first : first + width], window.indirect(entries))
+
+        def gather_scales(j, width):
+            for first in range(0, SLOTS, width):
+                gather(slot_s[0][:, j * SLOTS : (j + 1) * SLOTS], x_s[:, j * T : (j + 1) * T], first, width)
+
+        def gather_words(s, width):
+            for first in range(0, SLOTS, width):
+                gather(slot_w[:, s * SLOTS : (s + 1) * SLOTS], x_w[s][:].bitcast(U32), first, width)
+
+        nc.sync.dma_start(offsets[:], offs)
+        load_tokens(0)
+        load_pass("w1", w1_w, w1_words, 0)
+        load_token_scales()
+        load_weight_scales(w1_s, w1_scales)
+        load_pass("w3", w3_w, w3_words, 0)
+        load_weight_scales(w3_s, w3_scales)
+        load_tokens(1)
+        load_pass("w1", w1_w, w1_words, 1)
+        load_pass("w3", w3_w, w3_words, 1)
+        load_tokens(2)
+        gather_scales(0, C)
+        gather_scales(1, SLOTS)
+        nc.sync.dma_start(
+            out=slot_s[1][:].bitcast(I32)[0:PLANE_SPAN, :],
+            in_=slot_s[0][:].bitcast(I32)[BELOW : BELOW + PLANE_SPAN, :],
+        )
+        load_pass("w1", w1_w, w1_words, 2)
+        load_expert("w3", w3_w, w3_words, 0, 2, 2)
+        load_tokens(LAST)
+        load_expert("w1", w1_w, w1_words, 0, LAST, LAST)
+        load_expert("w3", w3_w, w3_words, 0, LAST, LAST)
+        load_expert("w1", w1_w, w1_words, 1, LAST, LAST)
+        load_expert("w3", w3_w, w3_words, 1, 2, LAST)
+        load_weight_scales(w2_s, w2_scales)
+        nc.sync.dma_start(out=w2_w[:].bitcast(I32), in_=w2_words[:, 0].bitcast(I32).rearrange("g p c -> p g c"))
+
+        for s in range(PASSES):
+            gather_words(s, P if s == LAST else C)
+
+        def first_product(bank, loaded, plane, t, s):
+            e = t // RANKS
+            group = e * PASSES + s
+            column = (s % HALF) * SLOTS + t * P
             nc.tensor.matmul_mx(
                 out=bank[t][:],
                 lhsT=slot_w[:, s * SLOTS + t * P : s * SLOTS + (t + 1) * P].bitcast(FP8X4),
-                lhsT_scale=slot_s[s // HALF][:, (s % HALF) * SLOTS + t * P : (s % HALF) * SLOTS + (t + 1) * P],
-                rhs=words_of[name, t // RANKS, s].bitcast(FP4X4),
-                rhs_scale=scales_of[name, t // RANKS, s],
+                lhsT_scale=slot_s[s // HALF][:, column : column + P],
+                rhs=loaded[e, s].bitcast(FP4X4),
+                rhs_scale=plane[:, group * H : (group + 1) * H],
                 start=(s == 0),
-                stop=(s == PASSES - 1),
+                stop=(s == LAST),
             )
 
         def pass_a(t, s):
-            first_product(a_bank, "w1", t, s)
+            first_product(a_bank, w1_w, w1_s, t, s)
 
         def pass_b(t, s):
-            first_product(b_bank, "w3", t, s)
+            first_product(b_bank, w3_w, w3_s, t, s)
 
         def by_pairs(ap):
             return ap.rearrange("p (u m v) -> p u m v", u=2, v=2)
@@ -118,152 +165,67 @@ def tile_moe_pke_glu_relu_kernel(
         def from_i_order(ap):
             return ap.rearrange("p (m u v) -> p u m v", u=2, v=2)
 
-        relu_a = [keep.tile([P, H], F32, name="relu_a%d" % t) for t in range(TILES)]
-        h = [sbuf([P, H], BF16, "h%d" % t) for t in range(TILES)]
-
         def relu(t):
             nc.scalar.activation(by_pairs(relu_a[t][:]), from_i_order(a_bank[t][:]), RELU)
 
         def product(t):
-            nc.vector.tensor_tensor(by_pairs(h[t][:]), from_i_order(b_bank[t][:]), by_pairs(relu_a[t][:]), MULT)
-
-        quantised = {}
-
-        def turn(tiles, copier, bank):
-            first, count = tiles[0], len(tiles)
-            for i, t in enumerate(tiles):
-                pairs = h[t][:].bitcast(F32)
-                for u in range(2):
-                    column = (2 * i + u) * P
-                    nc.tensor.transpose(bank[:, column : column + P], pairs[:, u * P : (u + 1) * P], ident[:])
-            turned = sbuf([P, count * H], BF16, "h_turned%d" % first)
-            copier(
-                turned[:].bitcast(F32).rearrange("p (i j u) -> p i j u", i=count, u=2),
-                bank[:, 0 : count * 2 * P].rearrange("p (i u j) -> p i j u", i=count, u=2),
-            )
-            h_w = sbuf([P, count * P], U32, "h_w%d" % first)
-            h_s = sbuf([P, count * P], U8, "h_s%d" % first)
-            nc.vector.quantize_mx(out=h_w[:].bitcast(FP8X4), scales=h_s[:], in_=turned[:])
-            quantised[first] = (h_w, h_s)
-
-        def second_product(tiles, copier, queue):
-            first, count = tiles[0], len(tiles)
-            e, rank = divmod(first, RANKS)
-            h_w, h_s = quantised[first]
-            nc.tensor.matmul_mx(
-                out=b_bank[first][:, 0 : count * P],
-                lhsT=w2_w[:, e, :].bitcast(FP4X4),
-                lhsT_scale=w2_s[:, e * N : (e + 1) * N],
-                rhs=h_w[:].bitcast(FP8X4),
-                rhs_scale=h_s[:],
-                start=True,
-                stop=True,
-            )
-            y = sbuf([P, count, P], F32, "y%d" % first)
-            copier(y[:], b_bank[first][:, 0 : count * P].rearrange("p (i j) -> p i j", i=count))
-            by_rank = out.rearrange("n (r e u) -> n r e u", r=RANKS, e=E)
-            queue.dma_start(out=by_rank[:, rank : rank + count, e, :], in_=y[:])
-
-        def load_token_scales(rows):
-            for r in rows:
-                nc.sync.dma_start(
-                    out=x_s[:].bitcast(I32)[r:P:BELOW, :].rearrange("p (j c) -> p j c", j=HALF),
-                    in_=x_scales.bitcast(I32)[:, r:SCALE_ROWS:4, :].rearrange("s q c -> q s c"),
+            halves = [slice(0, 1), slice(1, 2)] if t == TILES - 1 else [slice(0, 2)]
+            for u in halves:
+                nc.vector.tensor_tensor(
+                    by_pairs(h[t][:])[:, u], from_i_order(b_bank[t][:])[:, u], by_pairs(relu_a[t][:])[:, u], MULT
                 )
 
-        def gather_scales(j, first, last):
-            gather(slot_s[0][:, j * SLOTS + first : j * SLOTS + last], x_s[:, j * T : (j + 1) * T], first, last)
-
-        def load_weight_scales(queue, plane, source, experts, passes):
-            step = passes[1] - passes[0]
-            groups = source.rearrange("e s q c -> (e s) q c")
-            rows = groups[experts[0] * PASSES + passes[0] : (experts[-1] + 1) * PASSES : step]
-            load_scale_rows(queue, plane[:].rearrange("p e (s c) -> p (e s) c", c=H), rows)
-
-        def move_scales_up(queue):
-            queue.dma_start(
-                out=slot_s[1][:].bitcast(I32)[0:LIVE_SPAN, :],
-                in_=slot_s[0][:].bitcast(I32)[BELOW : BELOW + LIVE_SPAN, :],
-            )
-
-        def load_w2_scales():
-            load_scale_rows(
-                nc.sync, w2_s[:].rearrange("p (e c) -> p e c", e=E), w2_scales.rearrange("e s q c -> (e s) q c")
-            )
-
-        def load_w2_words():
-            nc.sync.dma_start(out=w2_w[:].bitcast(I32), in_=w2_words[:, 0].bitcast(I32).rearrange("g p c -> p g c"))
-
-        both, early, late, every = [0, 1], [0, 1], [2, 3], [0, 1, 2, 3]
-        w1_plane = weight_plane("w1", both, every)
-        w3_plane = weight_plane("w3", both, every)
-        zero(nc.gpsimd, x_s)
-        for plane in (w1_plane, w3_plane, w2_s, slot_s[1]):
-            zero(nc.vector, plane)
-        make_identity(nc, ident[:])
-
-        def by_pass(s):
-            return [(e, s) for e in both]
-
-        def by_expert(e, passes):
-            return [(e, s) for s in passes]
-
-        nc.sync.dma_start(offsets[:], offs)
-        load_tokens(0)
-        load_words("w1", w1_words, by_pass(0))
-        load_token_scales(range(4))
-        load_weight_scales(nc.sync, w1_plane, w1_scales, both, every)
-        load_words("w3", w3_words, by_pass(0))
-        load_weight_scales(nc.sync, w3_plane, w3_scales, both, every)
-        load_tokens(1)
-        load_words("w1", w1_words, by_pass(1))
-        load_words("w3", w3_words, by_pass(1))
-        load_tokens(2)
-        for e in both:
-            gather_scales(0, e * C, (e + 1) * C)
-        gather_scales(1, 0, SLOTS)
-        move_scales_up(nc.sync)
-        last = PASSES - 1
-
-        def gather_pass(s, width):
-            for first in range(0, SLOTS, width):
-                gather_words(s, first, first + width)
-
-        load_words("w1", w1_words, by_pass(2))
-        load_words("w3", w3_words, [(0, 2)])
-        load_tokens(last)
-        load_words("w1", w1_words, [(0, last)])
-        load_words("w3", w3_words, [(0, last)])
-        load_words("w1", w1_words, [(1, last)])
-        load_words("w3", w3_words, by_expert(1, late))
-        load_w2_scales()
-        load_w2_words()
-
-        for s in every:
-            gather_pass(s, P if s == last else C)
-        for s in early:
+        expert_0, expert_1 = range(0, RANKS), range(RANKS, TILES)
+        for s in range(HALF):
             for one_pass in (pass_a, pass_b):
                 for t in range(TILES):
                     one_pass(t, s)
         for t in range(TILES):
             pass_a(t, 2)
-        for t in (0, 1):
+        for t in expert_0:
             pass_b(t, 2)
-        for t in (0, 1):
-            pass_a(t, last)
+        for t in expert_0:
+            pass_a(t, LAST)
             relu(t)
-        for t in (0, 1):
-            pass_b(t, last)
+        for t in expert_0:
+            pass_b(t, LAST)
             product(t)
-        for t in (2, 3):
-            pass_a(t, last)
+        for t in expert_1:
+            pass_a(t, LAST)
             relu(t)
-        for t in (2, 3):
-            for s in late:
+        for t in expert_1:
+            for s in range(2, PASSES):
                 pass_b(t, s)
             product(t)
-        groups = [([0, 1], a_bank[2]), ([2], a_bank[0]), ([3], a_bank[1])]
-        for tiles, bank in groups:
-            turn(tiles, nc.scalar.copy, bank)
-        for tiles, bank in groups:
-            second_product(tiles, nc.scalar.copy, nc.sync)
+
+        turn_bank = [a_bank[2], a_bank[0], a_bank[1], a_bank[3]]
+        h_w = []
+        h_s = []
+        for t in range(TILES):
+            pairs = h[t][:].bitcast(F32)
+            for u in range(2):
+                nc.tensor.transpose(turn_bank[t][:, u * P : (u + 1) * P], pairs[:, u * P : (u + 1) * P], ident[:])
+            h_turned = sbuf([P, H], BF16, "h_turned%d" % t)
+            nc.scalar.copy(
+                h_turned[:].bitcast(F32).rearrange("p (j u) -> p j u", u=2),
+                turn_bank[t][:, 0 : 2 * P].rearrange("p (u j) -> p j u", u=2),
+            )
+            h_w.append(sbuf([P, P], U32, "h_w%d" % t))
+            h_s.append(sbuf([P, P], U8, "h_s%d" % t))
+            nc.vector.quantize_mx(out=h_w[t][:].bitcast(FP8X4), scales=h_s[t][:], in_=h_turned[:])
+
+        for t in range(TILES):
+            e, rank = divmod(t, RANKS)
+            nc.tensor.matmul_mx(
+                out=b_bank[t][:, 0:P],
+                lhsT=w2_w[:, e, :].bitcast(FP4X4),
+                lhsT_scale=w2_s[:, e * N : (e + 1) * N],
+                rhs=h_w[t][:].bitcast(FP8X4),
+                rhs_scale=h_s[t][:],
+                start=True,
+                stop=True,
+            )
+            y = sbuf([P, P], F32, "y%d" % t)
+            nc.scalar.copy(y[:], b_bank[t][:, 0:P])
+            column = (rank * E + e) * P
+            nc.sync.dma_start(out=out[:, column : column + P], in_=y[:])

@@ -47,9 +47,10 @@ def tile_moe_pke_glu_relu_kernel(
 
         offsets = keep.tile([P, SLOTS // LIST_ROWS], U16, name="offsets")
         x_w = [sbuf([P, T], I32, "x_w%d" % s) for s in range(PASSES)]
-        x_s = sbuf([P, HALF * T], U8, "x_s")
+        x_s = sbuf([P, T], U8, "x_s")
         slot_w = sbuf([P, PASSES * SLOTS], U32, "slot_w")
-        slot_s = [sbuf([P, HALF * SLOTS], U8, "slot_s%d" % pair) for pair in range(2)]
+        slot_rows = sbuf([P, SLOTS], U8, "slot_rows")
+        slot_s = sbuf([P, PASSES * SLOTS], U8, "slot_s")
         w2_s = sbuf([P, E * N], U8, "w2_s")
         w2_w = sbuf([P, E, FP4_BYTES * N], U8, "w2_w")
         ident = sbuf([P, P], F32, "ident")
@@ -62,8 +63,7 @@ def tile_moe_pke_glu_relu_kernel(
         w1_w = {}
         w3_w = {}
 
-        nc.gpsimd.memset(x_s[:].bitcast(I32), 0)
-        for plane in (w1_s, w3_s, w2_s, slot_s[1]):
+        for plane in (x_s, w1_s, slot_s, w3_s, w2_s):
             nc.vector.memset(plane[:].bitcast(I32), 0)
         make_identity(nc, ident[:])
 
@@ -71,10 +71,16 @@ def tile_moe_pke_glu_relu_kernel(
             nc.sync.dma_start(out=x_w[s][:], in_=x_words[s].rearrange("p t r -> p (t r)").bitcast(I32))
 
         def load_token_scales():
-            for r in range(GROUP_ROWS):
+            nc.sync.dma_start(
+                out=x_s[:].bitcast(I32)[0:P:2, :],
+                in_=x_scales.bitcast(I32).rearrange("s q c -> q s c"),
+            )
+
+        def move_slot_scales():
+            for first in (0, 2 * QUADRANT, QUADRANT, 3 * QUADRANT):
                 nc.sync.dma_start(
-                    out=x_s[:].bitcast(I32)[r:P:BELOW, :].rearrange("p (j c) -> p j c", j=HALF),
-                    in_=x_scales.bitcast(I32)[:, r:SCALE_ROWS:GROUP_ROWS, :].rearrange("s q c -> q s c"),
+                    out=slot_s[:].bitcast(I32)[first : first + GROUP_ROWS, :].rearrange("r (s c) -> r s c", s=PASSES),
+                    in_=slot_rows[:].bitcast(I32)[first : first + QUADRANT : 2, :],
                 )
 
         def load_weight_scales(plane, scales):
@@ -101,31 +107,23 @@ def tile_moe_pke_glu_relu_kernel(
             entries = offsets[:, first // LIST_ROWS : (first + width) // LIST_ROWS]
             nc.vector.tensor_copy(dst[:, first : first + width], window.indirect(entries))
 
-        def gather_scales(j, width):
-            for first in range(0, SLOTS, width):
-                gather(slot_s[0][:, j * SLOTS : (j + 1) * SLOTS], x_s[:, j * T : (j + 1) * T], first, width)
-
         def gather_words(s, width):
             for first in range(0, SLOTS, width):
                 gather(slot_w[:, s * SLOTS : (s + 1) * SLOTS], x_w[s][:].bitcast(U32), first, width)
 
         nc.sync.dma_start(offsets[:], offs)
+        load_token_scales()
         load_tokens(0)
         load_pass("w1", w1_w, w1_words, 0)
-        load_token_scales()
         load_weight_scales(w1_s, w1_scales)
+        gather(slot_rows, x_s[:], 0, SLOTS)
+        move_slot_scales()
         load_pass("w3", w3_w, w3_words, 0)
         load_weight_scales(w3_s, w3_scales)
         load_tokens(1)
         load_pass("w1", w1_w, w1_words, 1)
         load_pass("w3", w3_w, w3_words, 1)
         load_tokens(2)
-        gather_scales(0, C)
-        gather_scales(1, SLOTS)
-        nc.sync.dma_start(
-            out=slot_s[1][:].bitcast(I32)[0:PLANE_SPAN, :],
-            in_=slot_s[0][:].bitcast(I32)[BELOW : BELOW + PLANE_SPAN, :],
-        )
         load_pass("w1", w1_w, w1_words, 2)
         load_expert("w3", w3_w, w3_words, 0, 2, 2)
         load_tokens(LAST)
@@ -142,11 +140,11 @@ def tile_moe_pke_glu_relu_kernel(
         def first_product(bank, loaded, plane, t, s):
             e = t // RANKS
             group = e * PASSES + s
-            column = (s % HALF) * SLOTS + t * P
+            column = s * SLOTS + t * P
             nc.tensor.matmul_mx(
                 out=bank[t][:],
                 lhsT=slot_w[:, s * SLOTS + t * P : s * SLOTS + (t + 1) * P].bitcast(FP8X4),
-                lhsT_scale=slot_s[s // HALF][:, column : column + P],
+                lhsT_scale=slot_s[:, column : column + P],
                 rhs=loaded[e, s].bitcast(FP4X4),
                 rhs_scale=plane[:, group * H : (group + 1) * H],
                 start=(s == 0),

@@ -31,6 +31,7 @@ GROUP_ROWS = 4
 BELOW = 16
 PLANE_SPAN = 3 * QUADRANT + GROUP_ROWS
 FP4_BYTES = 2
+WARM_UPS = 3
 ALIGN = 64
 
 
@@ -135,7 +136,7 @@ def tile_moe_pke_glu_relu_kernel(
         nc.sync.dma_start(out=w2_w[:].bitcast(I32), in_=w2_words[:, 0].bitcast(I32).rearrange("g p c -> p g c"))
 
         for s in range(PASSES):
-            gather_words(s, P if s == LAST else C)
+            gather_words(s, P if s in (0, LAST) else C)
 
         def first_product(bank, loaded, plane, t, s):
             e = t // RANKS
@@ -172,6 +173,17 @@ def tile_moe_pke_glu_relu_kernel(
                 nc.vector.tensor_tensor(
                     by_pairs(h[t][:])[:, u], from_i_order(b_bank[t][:])[:, u], by_pairs(relu_a[t][:])[:, u], MULT
                 )
+
+        for repeat in range(WARM_UPS):
+            nc.tensor.matmul_mx(
+                out=b_bank[TILES - 1][:],
+                lhsT=slot_w[:, 0:P].bitcast(FP8X4),
+                lhsT_scale=slot_rows[:, 0:P],
+                rhs=w1_w[0, 0].bitcast(FP4X4),
+                rhs_scale=slot_rows[:],
+                start=True,
+                stop=True,
+            )
 
         expert_0, expert_1 = range(0, RANKS), range(RANKS, TILES)
         for s in range(HALF):

@@ -31,6 +31,7 @@ GROUP_ROWS = 4
 BELOW = 16
 PLANE_SPAN = 3 * QUADRANT + GROUP_ROWS
 FP4_BYTES = 2
+EARLY = PASSES + 2
 WARM_UPS = 3
 ALIGN = 64
 
@@ -60,11 +61,12 @@ def tile_moe_pke_glu_relu_kernel(
         relu_a = [keep.tile([P, H], F32, name="relu_a%d" % t) for t in range(TILES)]
         h = [sbuf([P, H], BF16, "h%d" % t) for t in range(TILES)]
         w1_s = sbuf([P, E * PASSES * H], U8, "w1_s")
-        w3_s = sbuf([P, E * PASSES * H], U8, "w3_s")
+        w3_s = sbuf([P, EARLY * H], U8, "w3_s")
+        w3_late_s = sbuf([P, (E * PASSES - EARLY) * H], U8, "w3_late_s")
         w1_w = {}
         w3_w = {}
 
-        for plane in (x_s, w1_s, slot_s, w3_s, w2_s):
+        for plane in (x_s, w1_s, slot_s, w3_s, w3_late_s, w2_s):
             nc.vector.memset(plane[:].bitcast(I32), 0)
         make_identity(nc, ident[:])
 
@@ -84,12 +86,12 @@ def tile_moe_pke_glu_relu_kernel(
                     in_=slot_rows[:].bitcast(I32)[first : first + QUADRANT : 2, :],
                 )
 
-        def load_weight_scales(plane, scales):
+        def load_weight_scales(plane, scales, groups):
             rows = scales.rearrange("e s q c -> (e s) q c").bitcast(I32)
             for r in range(GROUP_ROWS):
                 nc.sync.dma_start(
                     out=plane[:].bitcast(I32)[r:P:QUADRANT, :].rearrange("q (g c) -> q g c", c=rows.shape[2]),
-                    in_=rows[:, r:SCALE_ROWS:GROUP_ROWS, :].rearrange("g q c -> q g c"),
+                    in_=rows[groups, r:SCALE_ROWS:GROUP_ROWS, :].rearrange("g q c -> q g c"),
                 )
 
         def load_words(name, loaded, rows, groups):
@@ -116,11 +118,11 @@ def tile_moe_pke_glu_relu_kernel(
         load_token_scales()
         load_tokens(0)
         load_pass("w1", w1_w, w1_words, 0)
-        load_weight_scales(w1_s, w1_scales)
+        load_weight_scales(w1_s, w1_scales, slice(0, E * PASSES))
         gather(slot_rows, x_s[:], 0, SLOTS)
         move_slot_scales()
         load_pass("w3", w3_w, w3_words, 0)
-        load_weight_scales(w3_s, w3_scales)
+        load_weight_scales(w3_s, w3_scales, slice(0, EARLY))
         load_tokens(1)
         load_pass("w1", w1_w, w1_words, 1)
         load_pass("w3", w3_w, w3_words, 1)
@@ -130,9 +132,10 @@ def tile_moe_pke_glu_relu_kernel(
         load_tokens(LAST)
         load_expert("w1", w1_w, w1_words, 0, LAST, LAST)
         load_expert("w3", w3_w, w3_words, 0, LAST, LAST)
+        load_weight_scales(w3_late_s, w3_scales, slice(EARLY, E * PASSES))
         load_expert("w1", w1_w, w1_words, 1, LAST, LAST)
         load_expert("w3", w3_w, w3_words, 1, 2, LAST)
-        load_weight_scales(w2_s, w2_scales)
+        load_weight_scales(w2_s, w2_scales, slice(0, E))
         nc.sync.dma_start(out=w2_w[:].bitcast(I32), in_=w2_words[:, 0].bitcast(I32).rearrange("g p c -> p g c"))
 
         for s in range(PASSES):
@@ -140,23 +143,30 @@ def tile_moe_pke_glu_relu_kernel(
 
         def first_product(bank, loaded, plane, t, s):
             e = t // RANKS
-            group = e * PASSES + s
             column = s * SLOTS + t * P
             nc.tensor.matmul_mx(
                 out=bank[t][:],
                 lhsT=slot_w[:, s * SLOTS + t * P : s * SLOTS + (t + 1) * P].bitcast(FP8X4),
                 lhsT_scale=slot_s[:, column : column + P],
                 rhs=loaded[e, s].bitcast(FP4X4),
-                rhs_scale=plane[:, group * H : (group + 1) * H],
+                rhs_scale=plane(e * PASSES + s),
                 start=(s == 0),
                 stop=(s == LAST),
             )
 
+        def w1_plane(group):
+            return w1_s[:, group * H : (group + 1) * H]
+
+        def w3_plane(group):
+            if group < EARLY:
+                return w3_s[:, group * H : (group + 1) * H]
+            return w3_late_s[:, (group - EARLY) * H : (group - EARLY + 1) * H]
+
         def pass_a(t, s):
-            first_product(a_bank, w1_w, w1_s, t, s)
+            first_product(a_bank, w1_w, w1_plane, t, s)
 
         def pass_b(t, s):
-            first_product(b_bank, w3_w, w3_s, t, s)
+            first_product(b_bank, w3_w, w3_plane, t, s)
 
         def by_pairs(ap):
             return ap.rearrange("p (u m v) -> p u m v", u=2, v=2)
@@ -208,7 +218,7 @@ def tile_moe_pke_glu_relu_kernel(
                 pass_b(t, s)
             product(t)
 
-        turn_bank = [a_bank[2], a_bank[0], a_bank[1], a_bank[3]]
+        turn_bank = [a_bank[2], a_bank[3], a_bank[0], a_bank[1]]
         h_w = []
         h_s = []
         for t in range(TILES):

@@ -32,7 +32,6 @@ BELOW = 16
 PLANE_SPAN = 3 * QUADRANT + GROUP_ROWS
 FP4_BYTES = 2
 EARLY = PASSES + 2
-WARM_UPS = 3
 ALIGN = 64
 
 
@@ -183,17 +182,6 @@ def tile_moe_pke_glu_relu_kernel(
                 nc.vector.tensor_tensor(
                     by_pairs(h[t][:])[:, u], from_i_order(b_bank[t][:])[:, u], by_pairs(relu_a[t][:])[:, u], MULT
                 )
-
-        for repeat in range(WARM_UPS):
-            nc.tensor.matmul_mx(
-                out=b_bank[TILES - 1][:],
-                lhsT=slot_w[:, 0:P].bitcast(FP8X4),
-                lhsT_scale=slot_rows[:, 0:P],
-                rhs=w1_w[0, 0].bitcast(FP4X4),
-                rhs_scale=slot_rows[:],
-                start=True,
-                stop=True,
-            )
 
         expert_0, expert_1 = range(0, RANKS), range(RANKS, TILES)
         for s in range(HALF):

@@ -28,10 +28,9 @@ LIST_ROWS = 16
 SCALE_ROWS = 16
 QUADRANT = 32
 GROUP_ROWS = 4
-BELOW = 16
-PLANE_SPAN = 3 * QUADRANT + GROUP_ROWS
+ROW_STEP = P // (PASSES * SCALE_ROWS)
 FP4_BYTES = 2
-EARLY = PASSES + 2
+EARLY = PASSES + HALF
 ALIGN = 64
 
 
@@ -59,13 +58,13 @@ def tile_moe_pke_glu_relu_kernel(
         b_bank = [psum.tile([P, H], F32, name="b_bank%d" % t) for t in range(TILES)]
         relu_a = [keep.tile([P, H], F32, name="relu_a%d" % t) for t in range(TILES)]
         h = [sbuf([P, H], BF16, "h%d" % t) for t in range(TILES)]
-        w1_s = sbuf([P, E * PASSES * H], U8, "w1_s")
-        w3_s = sbuf([P, EARLY * H], U8, "w3_s")
-        w3_late_s = sbuf([P, (E * PASSES - EARLY) * H], U8, "w3_late_s")
+        widths = (EARLY * H, (E * PASSES - EARLY) * H)
+        w1_s = [sbuf([P, width], U8, "w1_s%d" % part) for part, width in enumerate(widths)]
+        w3_s = [sbuf([P, width], U8, "w3_s%d" % part) for part, width in enumerate(widths)]
         w1_w = {}
         w3_w = {}
 
-        for plane in (x_s, w1_s, slot_s, w3_s, w3_late_s, w2_s):
+        for plane in (x_s, w1_s[0], slot_s, w3_s[0], w1_s[1], w3_s[1], w2_s):
             nc.vector.memset(plane[:].bitcast(I32), 0)
         make_identity(nc, ident[:])
 
@@ -74,7 +73,7 @@ def tile_moe_pke_glu_relu_kernel(
 
         def load_token_scales():
             nc.sync.dma_start(
-                out=x_s[:].bitcast(I32)[0:P:2, :],
+                out=x_s[:].bitcast(I32)[0:P:ROW_STEP, :],
                 in_=x_scales.bitcast(I32).rearrange("s q c -> q s c"),
             )
 
@@ -82,7 +81,7 @@ def tile_moe_pke_glu_relu_kernel(
             for first in (0, 2 * QUADRANT, QUADRANT, 3 * QUADRANT):
                 nc.sync.dma_start(
                     out=slot_s[:].bitcast(I32)[first : first + GROUP_ROWS, :].rearrange("r (s c) -> r s c", s=PASSES),
-                    in_=slot_rows[:].bitcast(I32)[first : first + QUADRANT : 2, :],
+                    in_=slot_rows[:].bitcast(I32)[first : first + QUADRANT : ROW_STEP, :],
                 )
 
         def load_weight_scales(plane, scales, groups):
@@ -113,25 +112,28 @@ def tile_moe_pke_glu_relu_kernel(
             for first in range(0, SLOTS, width):
                 gather(slot_w[:, s * SLOTS : (s + 1) * SLOTS], x_w[s][:].bitcast(U32), first, width)
 
+        early, late = slice(0, EARLY), slice(EARLY, E * PASSES)
         nc.sync.dma_start(offsets[:], offs)
         load_token_scales()
         load_tokens(0)
         load_pass("w1", w1_w, w1_words, 0)
-        load_weight_scales(w1_s, w1_scales, slice(0, E * PASSES))
+        load_weight_scales(w1_s[0], w1_scales, early)
         gather(slot_rows, x_s[:], 0, SLOTS)
         move_slot_scales()
         load_pass("w3", w3_w, w3_words, 0)
-        load_weight_scales(w3_s, w3_scales, slice(0, EARLY))
+        load_weight_scales(w3_s[0], w3_scales, early)
         load_tokens(1)
         load_pass("w1", w1_w, w1_words, 1)
         load_pass("w3", w3_w, w3_words, 1)
         load_tokens(2)
-        load_pass("w1", w1_w, w1_words, 2)
+        load_expert("w1", w1_w, w1_words, 0, 2, 2)
+        load_weight_scales(w1_s[1], w1_scales, late)
+        load_expert("w1", w1_w, w1_words, 1, 2, 2)
         load_expert("w3", w3_w, w3_words, 0, 2, 2)
         load_tokens(LAST)
         load_expert("w1", w1_w, w1_words, 0, LAST, LAST)
         load_expert("w3", w3_w, w3_words, 0, LAST, LAST)
-        load_weight_scales(w3_late_s, w3_scales, slice(EARLY, E * PASSES))
+        load_weight_scales(w3_s[1], w3_scales, late)
         load_expert("w1", w1_w, w1_words, 1, LAST, LAST)
         load_expert("w3", w3_w, w3_words, 1, 2, LAST)
         load_weight_scales(w2_s, w2_scales, slice(0, E))
@@ -140,32 +142,25 @@ def tile_moe_pke_glu_relu_kernel(
         for s in range(PASSES):
             gather_words(s, P if s in (0, LAST) else C)
 
-        def first_product(bank, loaded, plane, t, s):
+        def first_product(bank, loaded, planes, t, s):
             e = t // RANKS
+            part, group = divmod(e * PASSES + s, EARLY)
             column = s * SLOTS + t * P
             nc.tensor.matmul_mx(
                 out=bank[t][:],
-                lhsT=slot_w[:, s * SLOTS + t * P : s * SLOTS + (t + 1) * P].bitcast(FP8X4),
+                lhsT=slot_w[:, column : column + P].bitcast(FP8X4),
                 lhsT_scale=slot_s[:, column : column + P],
                 rhs=loaded[e, s].bitcast(FP4X4),
-                rhs_scale=plane(e * PASSES + s),
+                rhs_scale=planes[part][:, group * H : (group + 1) * H],
                 start=(s == 0),
                 stop=(s == LAST),
             )
 
-        def w1_plane(group):
-            return w1_s[:, group * H : (group + 1) * H]
-
-        def w3_plane(group):
-            if group < EARLY:
-                return w3_s[:, group * H : (group + 1) * H]
-            return w3_late_s[:, (group - EARLY) * H : (group - EARLY + 1) * H]
-
         def pass_a(t, s):
-            first_product(a_bank, w1_w, w1_plane, t, s)
+            first_product(a_bank, w1_w, w1_s, t, s)
 
         def pass_b(t, s):
-            first_product(b_bank, w3_w, w3_plane, t, s)
+            first_product(b_bank, w3_w, w3_s, t, s)
 
         def by_pairs(ap):
             return ap.rearrange("p (u m v) -> p u m v", u=2, v=2)

@@ -31,7 +31,7 @@ GROUP_ROWS = 4
 ROW_STEP = P // (PASSES * SCALE_ROWS)
 FP4_BYTES = 2
 EARLY = PASSES + HALF
-ALIGN = 64
+ALIGN = 256
 
 
 def tile_moe_pke_glu_relu_kernel(

@@ -120,8 +120,8 @@ def tile_moe_pke_glu_relu_kernel(
         load_weight_scales(w1_s[0], w1_scales, early)
         gather(slot_rows, x_s[:], 0, SLOTS)
         move_slot_scales()
-        load_pass("w3", w3_w, w3_words, 0)
         load_weight_scales(w3_s[0], w3_scales, early)
+        load_pass("w3", w3_w, w3_words, 0)
         load_tokens(1)
         load_pass("w1", w1_w, w1_words, 1)
         load_pass("w3", w3_w, w3_words, 1)

@@ -42,18 +42,17 @@ def tile_moe_pke_glu_relu_kernel(
         keep = ctx.enter_context(tc.tile_pool(name="keep", bufs=1))
         psum = ctx.enter_context(tc.psum_pool(name="psum", bufs=1))
 
-        def sbuf(shape, dtype, name):
-            return keep.tile(shape, dtype, name=name, align_bytes=ALIGN)
+        def sbuf(shape, dtype, name, tag=None):
+            return keep.tile(shape, dtype, name=name, tag=tag or name, align_bytes=ALIGN)
 
         offsets = keep.tile([P, SLOTS // LIST_ROWS], U16, name="offsets")
         x_w = [sbuf([P, T], I32, "x_w%d" % s) for s in range(PASSES)]
-        x_s = sbuf([P, T], U8, "x_s")
+        x_s = sbuf([P, T], U8, "x_s", "x_s_then_ident")
         slot_w = sbuf([P, PASSES * SLOTS], U32, "slot_w")
         slot_rows = sbuf([P, SLOTS], U8, "slot_rows")
         slot_s = sbuf([P, PASSES * SLOTS], U8, "slot_s")
         w2_s = sbuf([P, E * N], U8, "w2_s")
         w2_w = sbuf([P, E, FP4_BYTES * N], U8, "w2_w")
-        ident = sbuf([P, P], F32, "ident")
         a_bank = [psum.tile([P, H], F32, name="a_bank%d" % t) for t in range(TILES)]
         b_bank = [psum.tile([P, H], F32, name="b_bank%d" % t) for t in range(TILES)]
         relu_a = [keep.tile([P, H], F32, name="relu_a%d" % t) for t in range(TILES)]
@@ -66,7 +65,6 @@ def tile_moe_pke_glu_relu_kernel(
 
         for plane in (x_s, w1_s[0], slot_s, w3_s[0], w1_s[1], w3_s[1], w2_s):
             nc.vector.memset(plane[:].bitcast(I32), 0)
-        make_identity(nc, ident[:])
 
         def load_tokens(s):
             nc.sync.dma_start(out=x_w[s][:], in_=x_words[s].rearrange("p t r -> p (t r)").bitcast(I32))
@@ -119,6 +117,8 @@ def tile_moe_pke_glu_relu_kernel(
         load_pass("w1", w1_w, w1_words, 0)
         load_weight_scales(w1_s[0], w1_scales, early)
         gather(slot_rows, x_s[:], 0, SLOTS)
+        ident = sbuf([P, P], F32, "ident", "x_s_then_ident")
+        make_identity(nc, ident[:])
         move_slot_scales()
         load_weight_scales(w3_s[0], w3_scales, early)
         load_pass("w3", w3_w, w3_words, 0)
@@ -127,9 +127,9 @@ def tile_moe_pke_glu_relu_kernel(
         load_pass("w3", w3_w, w3_words, 1)
         load_tokens(2)
         load_expert("w1", w1_w, w1_words, 0, 2, 2)
+        load_expert("w3", w3_w, w3_words, 0, 2, 2)
         load_weight_scales(w1_s[1], w1_scales, late)
         load_expert("w1", w1_w, w1_words, 1, 2, 2)
-        load_expert("w3", w3_w, w3_words, 0, 2, 2)
         load_tokens(LAST)
         load_expert("w1", w1_w, w1_words, 0, LAST, LAST)
         load_expert("w3", w3_w, w3_words, 0, LAST, LAST)
@@ -140,7 +140,7 @@ def tile_moe_pke_glu_relu_kernel(
         nc.sync.dma_start(out=w2_w[:].bitcast(I32), in_=w2_words[:, 0].bitcast(I32).rearrange("g p c -> p g c"))
 
         for s in range(PASSES):
-            gather_words(s, P if s in (0, LAST) else C)
+            gather_words(s, C if s == 2 else P)
 
         def first_product(bank, loaded, planes, t, s):
             e = t // RANKS
@@ -183,10 +183,12 @@ def tile_moe_pke_glu_relu_kernel(
             for one_pass in (pass_a, pass_b):
                 for t in range(TILES):
                     one_pass(t, s)
-        for t in range(TILES):
+        for t in expert_0:
             pass_a(t, 2)
         for t in expert_0:
             pass_b(t, 2)
+        for t in expert_1:
+            pass_a(t, 2)
         for t in expert_0:
             pass_a(t, LAST)
             relu(t)
@@ -209,13 +211,20 @@ def tile_moe_pke_glu_relu_kernel(
             for u in range(2):
                 nc.tensor.transpose(turn_bank[t][:, u * P : (u + 1) * P], pairs[:, u * P : (u + 1) * P], ident[:])
             h_turned = sbuf([P, H], BF16, "h_turned%d" % t)
-            nc.scalar.copy(
-                h_turned[:].bitcast(F32).rearrange("p (j u) -> p j u", u=2),
-                turn_bank[t][:, 0 : 2 * P].rearrange("p (u j) -> p j u", u=2),
-            )
             h_w.append(sbuf([P, P], U32, "h_w%d" % t))
             h_s.append(sbuf([P, P], U8, "h_s%d" % t))
-            nc.vector.quantize_mx(out=h_w[t][:].bitcast(FP8X4), scales=h_s[t][:], in_=h_turned[:])
+            width = P // 2 if t == TILES - 1 else P
+            for first in range(0, P, width):
+                slots = slice(first, first + width)
+                nc.scalar.copy(
+                    h_turned[:].bitcast(F32).rearrange("p (j u) -> p j u", u=2)[:, slots],
+                    turn_bank[t][:, 0 : 2 * P].rearrange("p (u j) -> p j u", u=2)[:, slots],
+                )
+                nc.vector.quantize_mx(
+                    out=h_w[t][:, slots].bitcast(FP8X4),
+                    scales=h_s[t][:, slots],
+                    in_=h_turned[:, 4 * first : 4 * (first + width)],
+                )
 
         for t in range(TILES):
             e, rank = divmod(t, RANKS)

@@ -28,7 +28,6 @@ LIST_ROWS = 16
 SCALE_ROWS = 16
 QUADRANT = 32
 GROUP_ROWS = 4
-ROW_STEP = P // (PASSES * SCALE_ROWS)
 FP4_BYTES = 2
 EARLY = PASSES + HALF
 ALIGN = 256
@@ -47,11 +46,11 @@ def tile_moe_pke_glu_relu_kernel(
 
         offsets = keep.tile([P, SLOTS // LIST_ROWS], U16, name="offsets")
         x_w = [sbuf([P, T], I32, "x_w%d" % s) for s in range(PASSES)]
-        x_s = sbuf([P, T], U8, "x_s", "x_s_then_ident")
+        x_s = sbuf([P, PASSES * T], U8, "x_s")
         slot_w = sbuf([P, PASSES * SLOTS], U32, "slot_w")
-        slot_rows = sbuf([P, SLOTS], U8, "slot_rows")
-        slot_s = sbuf([P, PASSES * SLOTS], U8, "slot_s")
+        slot_s = {}
         w2_s = sbuf([P, E * N], U8, "w2_s")
+        ident = sbuf([P, P], F32, "ident")
         w2_w = sbuf([P, E, FP4_BYTES * N], U8, "w2_w")
         a_bank = [psum.tile([P, H], F32, name="a_bank%d" % t) for t in range(TILES)]
         b_bank = [psum.tile([P, H], F32, name="b_bank%d" % t) for t in range(TILES)]
@@ -63,32 +62,25 @@ def tile_moe_pke_glu_relu_kernel(
         w1_w = {}
         w3_w = {}
 
-        for plane in (x_s, w1_s[0], slot_s, w3_s[0], w1_s[1], w3_s[1], w2_s):
+        for plane in (x_s, w1_s[0], w3_s[0]):
             nc.vector.memset(plane[:].bitcast(I32), 0)
+        for plane in (w1_s[1], w3_s[1], w2_s):
+            nc.gpsimd.memset(plane[:].bitcast(I32), 0)
+        make_identity(nc, ident[:])
 
         def load_tokens(s):
             nc.sync.dma_start(out=x_w[s][:], in_=x_words[s].rearrange("p t r -> p (t r)").bitcast(I32))
 
-        def load_token_scales():
-            nc.sync.dma_start(
-                out=x_s[:].bitcast(I32)[0:P:ROW_STEP, :],
-                in_=x_scales.bitcast(I32).rearrange("s q c -> q s c"),
-            )
-
-        def move_slot_scales():
-            for first in (0, 2 * QUADRANT, QUADRANT, 3 * QUADRANT):
-                nc.sync.dma_start(
-                    out=slot_s[:].bitcast(I32)[first : first + GROUP_ROWS, :].rearrange("r (s c) -> r s c", s=PASSES),
-                    in_=slot_rows[:].bitcast(I32)[first : first + QUADRANT : ROW_STEP, :],
-                )
-
-        def load_weight_scales(plane, scales, groups):
-            rows = scales.rearrange("e s q c -> (e s) q c").bitcast(I32)
+        def load_scales(plane, scales, groups):
+            rows = scales.bitcast(I32)
             for r in range(GROUP_ROWS):
                 nc.sync.dma_start(
                     out=plane[:].bitcast(I32)[r:P:QUADRANT, :].rearrange("q (g c) -> q g c", c=rows.shape[2]),
                     in_=rows[groups, r:SCALE_ROWS:GROUP_ROWS, :].rearrange("g q c -> q g c"),
                 )
+
+        def load_weight_scales(plane, scales, groups):
+            load_scales(plane, scales.rearrange("e s q c -> (e s) q c"), groups)
 
         def load_words(name, loaded, rows, groups):
             tile = sbuf([P, len(groups), FP4_BYTES * H], U8, "%s_w%d%d" % (name, groups[0][0], groups[0][1]))
@@ -104,23 +96,27 @@ def tile_moe_pke_glu_relu_kernel(
 
         def gather(dst, window, first, width):
             entries = offsets[:, first // LIST_ROWS : (first + width) // LIST_ROWS]
-            nc.vector.tensor_copy(dst[:, first : first + width], window.indirect(entries))
+            nc.vector.tensor_copy(dst, window.indirect(entries))
 
         def gather_words(s, width):
             for first in range(0, SLOTS, width):
-                gather(slot_w[:, s * SLOTS : (s + 1) * SLOTS], x_w[s][:].bitcast(U32), first, width)
+                column = s * SLOTS + first
+                gather(slot_w[:, column : column + width], x_w[s][:].bitcast(U32), first, width)
+
+        def gather_scales(s, experts, tag=None):
+            plane = sbuf([P, len(experts) * C], U8, "slot_s%d%d" % (s, experts[0]), tag)
+            gather(plane[:], x_s[:, s * T : (s + 1) * T], experts[0] * C, len(experts) * C)
+            for place, e in enumerate(experts):
+                slot_s[e, s] = plane[:, place * C : (place + 1) * C]
 
         early, late = slice(0, EARLY), slice(EARLY, E * PASSES)
         nc.sync.dma_start(offsets[:], offs)
-        load_token_scales()
         load_tokens(0)
-        load_pass("w1", w1_w, w1_words, 0)
+        load_expert("w1", w1_w, w1_words, 0, 0, 0)
+        load_scales(x_s, x_scales, slice(0, PASSES))
         load_weight_scales(w1_s[0], w1_scales, early)
-        gather(slot_rows, x_s[:], 0, SLOTS)
-        ident = sbuf([P, P], F32, "ident", "x_s_then_ident")
-        make_identity(nc, ident[:])
-        move_slot_scales()
         load_weight_scales(w3_s[0], w3_scales, early)
+        load_expert("w1", w1_w, w1_words, 1, 0, 0)
         load_pass("w3", w3_w, w3_words, 0)
         load_tokens(1)
         load_pass("w1", w1_w, w1_words, 1)
@@ -139,17 +135,25 @@ def tile_moe_pke_glu_relu_kernel(
         load_weight_scales(w2_s, w2_scales, slice(0, E))
         nc.sync.dma_start(out=w2_w[:].bitcast(I32), in_=w2_words[:, 0].bitcast(I32).rearrange("g p c -> p g c"))
 
-        for s in range(PASSES):
-            gather_words(s, C if s == 2 else P)
+        gather_words(0, P)
+        gather_scales(0, [0])
+        gather_scales(0, [1])
+        gather_scales(1, [0, 1])
+        gather_scales(2, [0, 1])
+        gather_words(1, P)
+        gather_scales(LAST, [0], "x_w1")
+        gather_words(2, C)
+        gather_scales(LAST, [1], "x_w2")
+        gather_words(LAST, P)
 
         def first_product(bank, loaded, planes, t, s):
-            e = t // RANKS
+            e, rank = divmod(t, RANKS)
             part, group = divmod(e * PASSES + s, EARLY)
             column = s * SLOTS + t * P
             nc.tensor.matmul_mx(
                 out=bank[t][:],
                 lhsT=slot_w[:, column : column + P].bitcast(FP8X4),
-                lhsT_scale=slot_s[:, column : column + P],
+                lhsT_scale=slot_s[e, s][:, rank * P : (rank + 1) * P],
                 rhs=loaded[e, s].bitcast(FP4X4),
                 rhs_scale=planes[part][:, group * H : (group + 1) * H],
                 start=(s == 0),

@@ -115,12 +115,13 @@ def tile_moe_pke_glu_relu_kernel(
         load_expert("w1", w1_w, w1_words, 0, 0, 0)
         load_scales(x_s, x_scales, slice(0, PASSES))
         load_weight_scales(w1_s[0], w1_scales, early)
-        load_weight_scales(w3_s[0], w3_scales, early)
         load_expert("w1", w1_w, w1_words, 1, 0, 0)
+        load_weight_scales(w3_s[0], w3_scales, early)
         load_pass("w3", w3_w, w3_words, 0)
         load_tokens(1)
-        load_pass("w1", w1_w, w1_words, 1)
-        load_pass("w3", w3_w, w3_words, 1)
+        for e in range(E):
+            load_expert("w1", w1_w, w1_words, e, 1, 1)
+            load_expert("w3", w3_w, w3_words, e, 1, 1)
         load_tokens(2)
         load_expert("w1", w1_w, w1_words, 0, 2, 2)
         load_expert("w3", w3_w, w3_words, 0, 2, 2)
@@ -183,20 +184,20 @@ def tile_moe_pke_glu_relu_kernel(
                 )
 
         expert_0, expert_1 = range(0, RANKS), range(RANKS, TILES)
-        for s in range(HALF):
-            for one_pass in (pass_a, pass_b):
-                for t in range(TILES):
-                    one_pass(t, s)
-        for t in expert_0:
-            pass_a(t, 2)
-        for t in expert_0:
-            pass_b(t, 2)
+        for one_pass in (pass_a, pass_b):
+            for t in range(TILES):
+                one_pass(t, 0)
+        for tiles, s in ((expert_0, 1), (expert_1, 1), (expert_0, 2)):
+            for t in tiles:
+                pass_a(t, s)
+            for t in reversed(tiles):
+                pass_b(t, s)
         for t in expert_1:
             pass_a(t, 2)
         for t in expert_0:
             pass_a(t, LAST)
             relu(t)
-        for t in expert_0:
+        for t in reversed(expert_0):
             pass_b(t, LAST)
             product(t)
         for t in expert_1:

from contextlib import ExitStack

import concourse.mybir as mybir
from concourse.masks import make_identity

K, T, E, C, H, N = 2048, 768, 2, 256, 512, 128
FLOPS = 2 * E * C * (2 * K * H + H * N)

F32 = mybir.dt.float32
BF16 = mybir.dt.bfloat16
I32 = mybir.dt.int32
U32 = mybir.dt.uint32
U16 = mybir.dt.uint16
U8 = mybir.dt.uint8
FP8X4 = mybir.dt.float8_e4m3fn_x4
FP4X4 = mybir.dt.float4_e2m1fn_x4
RELU = mybir.ActivationFunctionType.Relu
MULT = mybir.AluOpType.mult

P = 128
PASSES = K // 512
LAST = PASSES - 1
HALF = PASSES // 2
RANKS = 2
SLOTS = E * C
TILES = SLOTS // P
LIST_ROWS = 16
SCALE_ROWS = 16
QUADRANT = 32
GROUP_ROWS = 4
FP4_BYTES = 2
EARLY = PASSES + HALF
ALIGN = 256


def tile_moe_pke_glu_relu_kernel(
    tc, x_words, x_scales, w1_words, w1_scales, w3_words, w3_scales, w2_words, w2_scales, offs, out
):
    nc = tc.nc
    with ExitStack() as ctx:
        keep = ctx.enter_context(tc.tile_pool(name="keep", bufs=1))
        psum = ctx.enter_context(tc.psum_pool(name="psum", bufs=1))

        def sbuf(shape, dtype, name, tag=None):
            return keep.tile(shape, dtype, name=name, tag=tag or name, align_bytes=ALIGN)

        offsets = keep.tile([P, SLOTS // LIST_ROWS], U16, name="offsets")
        x_w = [sbuf([P, T], I32, "x_w%d" % s) for s in range(PASSES)]
        x_s = sbuf([P, PASSES * T], U8, "x_s")
        slot_w = sbuf([P, PASSES * SLOTS], U32, "slot_w")
        slot_s = {}
        w2_s = sbuf([P, E * N], U8, "w2_s")
        ident = sbuf([P, P], F32, "ident")
        w2_w = sbuf([P, E, FP4_BYTES * N], U8, "w2_w")
        a_bank = [psum.tile([P, H], F32, name="a_bank%d" % t) for t in range(TILES)]
        b_bank = [psum.tile([P, H], F32, name="b_bank%d" % t) for t in range(TILES)]
        relu_a = [keep.tile([P, H], F32, name="relu_a%d" % t) for t in range(TILES)]
        h = [sbuf([P, H], BF16, "h%d" % t) for t in range(TILES)]
        widths = (EARLY * H, (E * PASSES - EARLY) * H)
        w1_s = [sbuf([P, width], U8, "w1_s%d" % part) for part, width in enumerate(widths)]
        w3_s = [sbuf([P, width], U8, "w3_s%d" % part) for part, width in enumerate(widths)]
        w1_w = {}
        w3_w = {}

        for plane in (x_s, w1_s[0], w3_s[0]):
            nc.vector.memset(plane[:].bitcast(I32), 0)
        for plane in (w1_s[1], w3_s[1], w2_s):
            nc.gpsimd.memset(plane[:].bitcast(I32), 0)
        make_identity(nc, ident[:])

        def load_tokens(s):
            nc.sync.dma_start(out=x_w[s][:], in_=x_words[s].rearrange("p t r -> p (t r)").bitcast(I32))

        def load_scales(plane, scales, groups):
            rows = scales.bitcast(I32)
            for r in range(GROUP_ROWS):
                nc.sync.dma_start(
                    out=plane[:].bitcast(I32)[r:P:QUADRANT, :].rearrange("q (g c) -> q g c", c=rows.shape[2]),
                    in_=rows[groups, r:SCALE_ROWS:GROUP_ROWS, :].rearrange("g q c -> q g c"),
                )

        def load_weight_scales(plane, scales, groups):
            load_scales(plane, scales.rearrange("e s q c -> (e s) q c"), groups)

        def load_words(name, loaded, rows, groups):
            tile = sbuf([P, len(groups), FP4_BYTES * H], U8, "%s_w%d%d" % (name, groups[0][0], groups[0][1]))
            nc.sync.dma_start(out=tile[:].bitcast(I32), in_=rows.bitcast(I32).rearrange("g p c -> p g c"))
            for g, group in enumerate(groups):
                loaded[group] = tile[:, g, :]

        def load_pass(name, loaded, words, s):
            load_words(name, loaded, words[:, s], [(e, s) for e in range(E)])

        def load_expert(name, loaded, words, e, first, last):
            load_words(name, loaded, words[e, first : last + 1], [(e, s) for s in range(first, last + 1)])

        def gather(dst, window, first, width):
            entries = offsets[:, first // LIST_ROWS : (first + width) // LIST_ROWS]
            nc.vector.tensor_copy(dst, window.indirect(entries))

        def gather_words(s, width):
            for first in range(0, SLOTS, width):
                column = s * SLOTS + first
                gather(slot_w[:, column : column + width], x_w[s][:].bitcast(U32), first, width)

        def gather_scales(s, experts, tag=None):
            plane = sbuf([P, len(experts) * C], U8, "slot_s%d%d" % (s, experts[0]), tag)
            gather(plane[:], x_s[:, s * T : (s + 1) * T], experts[0] * C, len(experts) * C)
            for place, e in enumerate(experts):
                slot_s[e, s] = plane[:, place * C : (place + 1) * C]

        early, late = slice(0, EARLY), slice(EARLY, E * PASSES)
        nc.sync.dma_start(offsets[:], offs)
        load_tokens(0)
        load_expert("w1", w1_w, w1_words, 0, 0, 0)
        load_scales(x_s, x_scales, slice(0, PASSES))
        load_weight_scales(w1_s[0], w1_scales, early)
        load_expert("w1", w1_w, w1_words, 1, 0, 0)
        load_weight_scales(w3_s[0], w3_scales, early)
        load_pass("w3", w3_w, w3_words, 0)
        load_tokens(1)
        for e in range(E):
            load_expert("w1", w1_w, w1_words, e, 1, 1)
            load_expert("w3", w3_w, w3_words, e, 1, 1)
        load_tokens(2)
        load_expert("w1", w1_w, w1_words, 0, 2, 2)
        load_expert("w3", w3_w, w3_words, 0, 2, 2)
        load_weight_scales(w1_s[1], w1_scales, late)
        load_expert("w1", w1_w, w1_words, 1, 2, 2)
        load_tokens(LAST)
        load_expert("w1", w1_w, w1_words, 0, LAST, LAST)
        load_expert("w3", w3_w, w3_words, 0, LAST, LAST)
        load_weight_scales(w3_s[1], w3_scales, late)
        load_expert("w1", w1_w, w1_words, 1, LAST, LAST)
        load_expert("w3", w3_w, w3_words, 1, 2, LAST)
        load_weight_scales(w2_s, w2_scales, slice(0, E))
        nc.sync.dma_start(out=w2_w[:].bitcast(I32), in_=w2_words[:, 0].bitcast(I32).rearrange("g p c -> p g c"))

        gather_words(0, P)
        gather_scales(0, [0])
        gather_scales(0, [1])
        gather_scales(1, [0, 1])
        gather_scales(2, [0, 1])
        gather_words(1, P)
        gather_scales(LAST, [0], "x_w1")
        gather_words(2, C)
        gather_scales(LAST, [1], "x_w2")
        gather_words(LAST, P)

        def first_product(bank, loaded, planes, t, s):
            e, rank = divmod(t, RANKS)
            part, group = divmod(e * PASSES + s, EARLY)
            column = s * SLOTS + t * P
            nc.tensor.matmul_mx(
                out=bank[t][:],
                lhsT=slot_w[:, column : column + P].bitcast(FP8X4),
                lhsT_scale=slot_s[e, s][:, rank * P : (rank + 1) * P],
                rhs=loaded[e, s].bitcast(FP4X4),
                rhs_scale=planes[part][:, group * H : (group + 1) * H],
                start=(s == 0),
                stop=(s == LAST),
            )

        def pass_a(t, s):
            first_product(a_bank, w1_w, w1_s, t, s)

        def pass_b(t, s):
            first_product(b_bank, w3_w, w3_s, t, s)

        def by_pairs(ap):
            return ap.rearrange("p (u m v) -> p u m v", u=2, v=2)

        def from_i_order(ap):
            return ap.rearrange("p (m u v) -> p u m v", u=2, v=2)

        def relu(t):
            nc.scalar.activation(by_pairs(relu_a[t][:]), from_i_order(a_bank[t][:]), RELU)

        def product(t):
            halves = [slice(0, 1), slice(1, 2)] if t == TILES - 1 else [slice(0, 2)]
            for u in halves:
                nc.vector.tensor_tensor(
                    by_pairs(h[t][:])[:, u], from_i_order(b_bank[t][:])[:, u], by_pairs(relu_a[t][:])[:, u], MULT
                )

        expert_0, expert_1 = range(0, RANKS), range(RANKS, TILES)
        for one_pass in (pass_a, pass_b):
            for t in range(TILES):
                one_pass(t, 0)
        for tiles, s in ((expert_0, 1), (expert_1, 1), (expert_0, 2)):
            for t in tiles:
                pass_a(t, s)
            for t in reversed(tiles):
                pass_b(t, s)
        for t in expert_1:
            pass_a(t, 2)
        for t in expert_0:
            pass_a(t, LAST)
            relu(t)
        for t in reversed(expert_0):
            pass_b(t, LAST)
            product(t)
        for t in expert_1:
            pass_a(t, LAST)
            relu(t)
        for t in expert_1:
            for s in range(2, PASSES):
                pass_b(t, s)
            product(t)

        turn_bank = [a_bank[2], a_bank[3], a_bank[0], a_bank[1]]
        h_w = []
        h_s = []
        for t in range(TILES):
            pairs = h[t][:].bitcast(F32)
            for u in range(2):
                nc.tensor.transpose(turn_bank[t][:, u * P : (u + 1) * P], pairs[:, u * P : (u + 1) * P], ident[:])
            h_turned = sbuf([P, H], BF16, "h_turned%d" % t)
            h_w.append(sbuf([P, P], U32, "h_w%d" % t))
            h_s.append(sbuf([P, P], U8, "h_s%d" % t))
            width = P // 2 if t == TILES - 1 else P
            for first in range(0, P, width):
                slots = slice(first, first + width)
                nc.scalar.copy(
                    h_turned[:].bitcast(F32).rearrange("p (j u) -> p j u", u=2)[:, slots],
                    turn_bank[t][:, 0 : 2 * P].rearrange("p (u j) -> p j u", u=2)[:, slots],
                )
                nc.vector.quantize_mx(
                    out=h_w[t][:, slots].bitcast(FP8X4),
                    scales=h_s[t][:, slots],
                    in_=h_turned[:, 4 * first : 4 * (first + width)],
                )

        for t in range(TILES):
            e, rank = divmod(t, RANKS)
            nc.tensor.matmul_mx(
                out=b_bank[t][:, 0:P],
                lhsT=w2_w[:, e, :].bitcast(FP4X4),
                lhsT_scale=w2_s[:, e * N : (e + 1) * N],
                rhs=h_w[t][:].bitcast(FP8X4),
                rhs_scale=h_s[t][:],
                start=True,
                stop=True,
            )
            y = sbuf([P, P], F32, "y%d" % t)
            nc.scalar.copy(y[:], b_bank[t][:, 0:P])
            column = (rank * E + e) * P
            nc.sync.dma_start(out=out[:, column : column + P], in_=y[:])
